import numpy as np
import ml_dtypes


def mxq(x, axis, fmt="e4m3"):
    dtype, down = {"e4m3": (ml_dtypes.float8_e4m3fn, 7), "e5m2": (ml_dtypes.float8_e5m2, 14)}[fmt]
    v = np.moveaxis(np.asarray(x, np.float32).astype(ml_dtypes.bfloat16).astype(np.float64), axis, -1)
    blocks = v.reshape(v.shape[:-1] + (-1, 32))
    amax = np.abs(blocks).max(-1, keepdims=True)
    byte = np.maximum(np.where(amax > 0, np.frexp(amax)[1] - 1 + 127, 0) - down, 1)
    scale = np.exp2(byte - 127.0)
    codes = (blocks / scale).astype(np.float32).astype(dtype).astype(np.float64)
    return np.moveaxis((codes * scale).reshape(v.shape), -1, axis)


WIDE = False


def mx_kscale(k):
    if not WIDE:
        return np.ones(k)
    levels = np.array([10, -10, 5, -5, 0])
    if k % 512:
        return np.exp2(np.random.permutation(np.resize(levels, k // 32))).repeat(32)
    a = np.empty((k // 512, 16))
    for p in range(k // 512):
        a[p, :8] = np.random.permutation(np.resize(levels, 8))
        for g in range(8):
            far = levels[np.abs(levels - a[p, g]) >= 10]
            a[p, g + 8] = far[np.random.randint(len(far))]
    return np.exp2(a.ravel()).repeat(32)


def f64(x):
    return np.asarray(x).astype(np.float64)


def striped(idx):
    return np.tile(idx.reshape(-1, 16).T, (8, 1)).astype(np.uint16)


def unstriped(offs):
    return offs[:16].T.reshape(-1).astype(np.int64)


def pack_weight(w):
    k, n = w.shape
    w = f64(np.asarray(w, np.float32).astype(ml_dtypes.bfloat16)).reshape(k // 32, 32, n)
    amax = np.abs(w).max(1)
    byte = np.clip(np.where(amax > 0, np.frexp(amax)[1] - 1 + 127 - 7, 1), 1, 254)
    scaled = (w * np.exp2(127.0 - byte)[:, None, :]).reshape(k, n).astype(np.float32)
    words = np.ascontiguousarray(scaled.reshape(k // 512, 128, 4, n).transpose(0, 1, 3, 2)).astype(ml_dtypes.float8_e4m3fn).view(np.uint8)
    return words, np.ascontiguousarray(byte.astype(np.uint8).reshape(k // 512, 16, n))


def unpack_weight(words, scales):
    g, p, n, _ = words.shape
    vals = np.ascontiguousarray(words).view(ml_dtypes.float8_e4m3fn).astype(np.float64) * np.repeat(np.exp2(scales.astype(np.float64) - 127.0), 8, axis=1)[..., None]
    return vals.transpose(0, 1, 3, 2).reshape(g * 512, n)


K, T, S, H, V, W = 1024, 2048, 512, 512, 256, 1024
P = 2 ** 7


def setup_inputs():
    n = np.random.standard_normal
    s = mx_kscale(K)[:, None]
    u = mx_kscale(H)
    packed_xT = pack_weight(n((K, T)) * s)
    packed_eT = pack_weight(n((H, W)) / np.sqrt(H) / u[:, None])
    return {
        "x_words": packed_xT[0],
        "x_scales": packed_xT[1],
        "w1": (n((K, H)) / np.sqrt(K) / s * u).astype(np.float32),
        "e_words": packed_eT[0],
        "e_scales": packed_eT[1],
        "qn": (np.tile(np.random.uniform(1.5, 3.0, W), (P, 1))).astype(np.float32),
        "own": (np.random.uniform(1.5, 3.0, (S, 1))).astype(np.float32),
        "mass": (np.tile(np.random.uniform(0.5, 1.5, V), (P, 1))).astype(np.float32),
        "inv": (np.tile(np.random.uniform(0.5, 2.0, V), (P, 1))).astype(np.float32),
        "offs": striped(np.random.permutation(T)[:S]),
        "cen": striped(np.random.permutation(W)[:V]),
    }


def reference(x_words, x_scales, w1, e_words, e_scales, qn, own, mass, inv, offs, cen):
    xq = unpack_weight(x_words, x_scales)[:, unstriped(offs)]
    h = mxq(f64(w1), 0, "e4m3").T @ xq
    e_cen = unpack_weight(e_words, e_scales)[:, unstriped(cen)]
    y = mxq(h, 0, "e4m3").T @ e_cen
    dd = f64(qn)[:1][:, unstriped(cen)] - (0.2 * y) + f64(own)
    gg = f64(mass)[:1] / (dd + 1.0)
    total = gg.sum(axis=1, keepdims=True)
    qq = gg / total
    rr = (qq * qq) * f64(inv)[:1]
    sum2 = rr.sum(axis=1, keepdims=True)
    return rr / sum2

@@ -1,0 +1,223 @@
+from contextlib import ExitStack
+
+import concourse.mybir as mybir
+from concourse.masks import make_identity
+
+K, T, S, H, V, W = 1024, 2048, 512, 512, 256, 1024
+FLOPS = 2 * K * H * S + 2 * H * S * V
+
+F32 = mybir.dt.float32
+BF16 = mybir.dt.bfloat16
+I32 = mybir.dt.int32
+U32 = mybir.dt.uint32
+U16 = mybir.dt.uint16
+U8 = mybir.dt.uint8
+FP8X4 = mybir.dt.float8_e4m3fn_x4
+ALU = mybir.AluOpType
+ACT = mybir.ActivationFunctionType
+AXIS = mybir.AxisListType
+
+P = 128
+PACK = 4
+K_PASS = P * PACK
+PASSES = K // K_PASS
+TILES = S // P
+M_SCALAR = 96
+
+
+def tile_picked_ydec_tgt_p_kernel(
+    tc, x_words, x_scales, w1, e_words, e_scales, qn, own, mass, inv, offs, cen, out
+):
+    nc = tc.nc
+    with ExitStack() as ctx:
+        keep = ctx.enter_context(tc.tile_pool(name="keep", bufs=1))
+        work = ctx.enter_context(tc.tile_pool(name="work", bufs=4))
+        psum = ctx.enter_context(tc.psum_pool(name="psum", bufs=4))
+
+        def kept(name, shape, dtype, tag=None):
+            return keep.tile(shape, dtype, name=name, tag=tag or name, align_bytes=64)
+
+        offs_sb = kept("offs_sb", [P, S // 16], U16)
+        cen_sb = kept("cen_sb", [P, V // 16], U16)
+        nc.sync.dma_start(offs_sb[:], offs)
+        nc.sync.dma_start(cen_sb[:], cen)
+
+        w_raw = [kept("w_raw%d" % g, [P, PACK, H], F32) for g in range(PASSES)]
+        for g in range(PASSES):
+            nc.sync.dma_start(w_raw[g][:], w1[g * K_PASS : (g + 1) * K_PASS, :].rearrange("(p j) c -> p j c", j=PACK))
+        x_table = [kept("x_table%d" % g, [P, T], U32) for g in range(PASSES)]
+        for g in range(PASSES):
+            nc.sync.dma_start(x_table[g][:].bitcast(I32), x_words[g].rearrange("p n t -> p (n t)").bitcast(I32))
+
+        xs_table = kept("xs_table", [P, T], U8)
+        nc.vector.memset(xs_table[:].bitcast(I32), 0)
+        rows = kept("rows", [P, V], F32)
+        nc.vector.memset(rows[:], 0.0)
+        qn_table = kept("qn_table", [P, W], F32)
+        nc.vector.memset(qn_table[:], 0.0)
+        es_table = kept("es_table", [P, W], U8)
+        nc.vector.memset(es_table[:].bitcast(I32), 0)
+
+        mass_row = kept("mass_row", [1, V], F32)
+        inv_row = kept("inv_row", [1, V], F32)
+        nc.scalar.dma_start(mass_row[:], mass[0:1, :])
+        nc.scalar.dma_start(inv_row[:], inv[0:1, :])
+        ident = kept("ident", [P, P], F32)
+        make_identity(nc, ident[:])
+        for q in range(4):
+            nc.scalar.dma_start(
+                xs_table[32 * q : 32 * q + 4 * PASSES, :].bitcast(I32),
+                x_scales[:, 4 * q : 4 * q + 4, :].bitcast(I32),
+            )
+        nc.gpsimd.dma_start(qn_table[0:1, :], qn[0:1, :])
+        nc.gpsimd.dma_start(rows[1 : 1 + TILES, 0:P], own.rearrange("(a m) o -> a (m o)", m=P))
+        for q in range(4):
+            nc.gpsimd.dma_start(
+                es_table[32 * q : 32 * q + 4, :].bitcast(I32), e_scales[0, 4 * q : 4 * q + 4, :].bitcast(I32)
+            )
+
+        mass_sum = kept("mass_sum", [1, 1], F32)
+        nc.vector.tensor_reduce(mass_sum[:], mass_row[:], AXIS.X, ALU.add, apply_absolute_value=True)
+        mass_root = kept("mass_root", [1, 1], F32)
+        nc.scalar.activation(mass_root[:], mass_sum[:], ACT.Abs_reciprocal_sqrt)
+        share = kept("share", [1, V], F32)
+        nc.vector.tensor_scalar(share[:], mass_row[:], mass_root[:], mass_root[:], ALU.mult, ALU.mult)
+        share_inv = kept("share_inv", [1, V], F32)
+        nc.vector.tensor_tensor(share_inv[:], share[:], inv_row[:], ALU.mult)
+        nc.vector.tensor_tensor(rows[0:1, :], share_inv[:], share[:], ALU.mult)
+
+        w_codes = [kept("w_codes%d" % g, [P, H], U32) for g in range(PASSES)]
+        w_scales = [kept("w_scales%d" % g, [P, H], U8) for g in range(PASSES)]
+        w_bf = [kept("w_bf%d" % g, [P, PACK * H], BF16) for g in range(PASSES)]
+
+        def round_w(g):
+            dst = w_bf[g][:].rearrange("p (t m j) -> p m t j", t=PACK, j=PACK)
+            src = w_raw[g][:].rearrange("p j (m t) -> p m t j", t=PACK)
+            nc.scalar.copy(dst[:, 0:M_SCALAR], src[:, 0:M_SCALAR])
+            nc.vector.tensor_copy(dst[:, M_SCALAR:P], src[:, M_SCALAR:P])
+
+        def quantize_w(g):
+            nc.vector.quantize_mx(out=w_codes[g][:].bitcast(FP8X4), scales=w_scales[g][:], in_=w_bf[g][:])
+
+        xs_pick = kept("xs_pick", [P, S], U8)
+        es_pick = kept("es_pick", [P, V], U8)
+        qn_pick = kept("qn_pick", [P, V], F32)
+        e_pick = kept("e_pick", [P, V], U32)
+
+        round_w(0)
+        e_table = kept("e_table", [P, W], U32, tag="w_raw0")
+        nc.sync.dma_start(e_table[:].bitcast(I32), e_words[0].rearrange("p n t -> p (n t)").bitcast(I32))
+        nc.vector.tensor_copy(qn_pick[:], qn_table[:].indirect(cen_sb[:]))
+        nc.vector.tensor_copy(xs_pick[:], xs_table[:].indirect(offs_sb[:]))
+        quantize_w(0)
+        round_w(1)
+        nc.vector.tensor_copy(es_pick[:], es_table[:].indirect(cen_sb[:]))
+
+        turn = psum.tile([P, 4, P], F32, name="turn", tag="y")
+        for b in range(2):
+            nc.tensor.transpose(turn[:, b, :], qn_pick[:, b * P : (b + 1) * P], ident[:])
+            nc.tensor.transpose(turn[:, 2 + b, :], rows[:, b * P : (b + 1) * P], ident[:])
+        cols = kept("cols", [P, 4], F32, tag="es_table")
+        nc.vector.tensor_copy(cols[:], turn[:, :, 0])
+        own1 = kept("own1", [P, TILES], F32)
+        nc.vector.tensor_scalar_add(own1[:], turn[:, 2, 1 : 1 + TILES], 1.0)
+        spread = psum.tile([P, 4, P], F32, name="spread", tag="y")
+        for b in range(4):
+            nc.tensor.transpose(spread[:, b, :], cols[:, b : b + 1].to_broadcast([P, P]), ident[:])
+        wide = kept("wide", [P, 2 * V], F32)
+        nc.vector.tensor_copy(wide[:], spread[:].rearrange("p b n -> p (b n)"))
+        qn_wide = wide[:, 0:V]
+        c_wide = wide[:, V : 2 * V]
+
+        quantize_w(1)
+        x_first = kept("x_first", [P, S], U32, tag="xs_table")
+        nc.vector.tensor_copy(x_first[:], x_table[0][:].indirect(offs_sb[:]))
+        h_banks = [psum.tile([P, PACK, P], F32, name="h", tag="h") for a in range(TILES)]
+
+        def h_pass(a, j, g):
+            cols_a = slice(a * P, (a + 1) * P)
+            moving = x_first[:, cols_a] if g == 0 else x_last[a // 2][:, (a % 2) * P : (a % 2 + 1) * P]
+            nc.tensor.matmul_mx(
+                out=h_banks[a][:, j, :],
+                lhsT=w_codes[g][:, j * P : (j + 1) * P].bitcast(FP8X4),
+                lhsT_scale=w_scales[g][:, j * P : (j + 1) * P],
+                rhs=moving.bitcast(FP8X4),
+                rhs_scale=xs_pick[4 * g : P, cols_a],
+                start=(g == 0),
+                stop=(g == PASSES - 1),
+            )
+
+        for a in range(TILES):
+            h_pass(a, 0, 0)
+        x_last = [kept("x_last0", [P, 256], U32, tag="es_table"), kept("x_last1", [P, 256], U32)]
+        for half in range(2):
+            nc.vector.tensor_copy(x_last[half][:], x_table[1][:].indirect(offs_sb[:, half * 16 : (half + 1) * 16]))
+        nc.vector.tensor_copy(e_pick[:], e_table[:].indirect(cen_sb[:]))
+
+        state = [dict() for a in range(TILES)]
+
+        def wt(a, name, shape, dtype):
+            state[a][name] = work.tile(shape, dtype, name=name, align_bytes=64)
+            return state[a][name]
+
+        def project(a):
+            h = h_banks[a]
+            for j in range(PACK):
+                for g in range(PASSES):
+                    if j or g:
+                        h_pass(a, j, g)
+            h_bf = wt(a, "h_bf", [P, P, PACK], BF16)
+            nc.scalar.copy(h_bf[:], h[:].rearrange("p j n -> p n j"))
+
+        def inner(a):
+            h_codes = wt(a, "h_codes", [P, P], U32)
+            h_scales = wt(a, "h_scales", [P, P], U8)
+            nc.vector.quantize_mx(
+                out=h_codes[:].bitcast(FP8X4), scales=h_scales[:], in_=state[a]["h_bf"][:].rearrange("p n j -> p (n j)")
+            )
+            y = psum.tile([P, 2 * V], F32, name="y", tag="y")
+            state[a]["y"] = y
+            nc.tensor.matmul_mx(
+                out=y[:, 0:V],
+                lhsT=h_codes[:].bitcast(FP8X4),
+                lhsT_scale=h_scales[:],
+                rhs=e_pick[:].bitcast(FP8X4),
+                rhs_scale=es_pick[:],
+                start=True,
+                stop=True,
+            )
+
+        def distance(a):
+            part = wt(a, "part", [P, V], F32)
+            nc.vector.scalar_tensor_tensor(part[:], state[a]["y"][:, 0:V], -0.2, qn_wide, ALU.mult, ALU.add)
+            root = wt(a, "root", [P, V], F32)
+            nc.scalar.activation(root[:], part[:], ACT.Abs_reciprocal_sqrt, bias=own1[:, a : a + 1])
+            kern = wt(a, "kern", [P, V], F32)
+            kern_sum = wt(a, "kern_sum", [P, 1], F32)
+            nc.scalar.activation(kern[:], root[:], ACT.Square, accum_out=kern_sum[:])
+
+        def weigh(a):
+            kern = state[a]["kern"]
+            norm = wt(a, "norm", [P, 1], F32)
+            nc.vector.reciprocal(norm[:], state[a]["kern_sum"][:])
+            left = wt(a, "left", [P, V], F32)
+            nc.vector.tensor_tensor(left[:], kern[:], c_wide, ALU.mult)
+            rr = wt(a, "rr", [P, V], F32)
+            rr_sum = wt(a, "rr_sum", [P, 1], F32)
+            nc.vector.scalar_tensor_tensor(rr[:], kern[:], norm[:], left[:], ALU.mult, ALU.mult, accum_out=rr_sum[:])
+
+        def finish(a):
+            norm2 = wt(a, "norm2", [P, 1], F32)
+            nc.vector.reciprocal(norm2[:], state[a]["rr_sum"][:])
+            res = wt(a, "res", [P, V], F32)
+            if a < TILES - 1:
+                nc.scalar.activation(res[:], state[a]["rr"][:], ACT.Copy, scale=norm2[:])
+            else:
+                nc.vector.tensor_scalar_mul(res[:], state[a]["rr"][:], norm2[:])
+            nc.sync.dma_start(out[a * P : (a + 1) * P, :], res[:])
+
+        stages = [project, inner, distance, weigh, finish]
+        for step in range(TILES + len(stages) - 1):
+            for s in reversed(range(len(stages))):
+                if 0 <= step - s < TILES:
+                    stages[s](step - s)

@@ -22,7 +22,6 @@ PACK = 4
 K_PASS = P * PACK
 PASSES = K // K_PASS
 TILES = S // P
-M_SCALAR = 96
 
 
 def tile_picked_ydec_tgt_p_kernel(
@@ -39,42 +38,51 @@ def tile_picked_ydec_tgt_p_kernel(
 
         offs_sb = kept("offs_sb", [P, S // 16], U16)
         cen_sb = kept("cen_sb", [P, V // 16], U16)
-        nc.sync.dma_start(offs_sb[:], offs)
-        nc.sync.dma_start(cen_sb[:], cen)
-
-        w_raw = [kept("w_raw%d" % g, [P, PACK, H], F32) for g in range(PASSES)]
-        for g in range(PASSES):
-            nc.sync.dma_start(w_raw[g][:], w1[g * K_PASS : (g + 1) * K_PASS, :].rearrange("(p j) c -> p j c", j=PACK))
-        x_table = [kept("x_table%d" % g, [P, T], U32) for g in range(PASSES)]
-        for g in range(PASSES):
-            nc.sync.dma_start(x_table[g][:].bitcast(I32), x_words[g].rearrange("p n t -> p (n t)").bitcast(I32))
-
-        xs_table = kept("xs_table", [P, T], U8)
-        nc.vector.memset(xs_table[:].bitcast(I32), 0)
-        rows = kept("rows", [P, V], F32)
-        nc.vector.memset(rows[:], 0.0)
-        qn_table = kept("qn_table", [P, W], F32)
-        nc.vector.memset(qn_table[:], 0.0)
-        es_table = kept("es_table", [P, W], U8)
-        nc.vector.memset(es_table[:].bitcast(I32), 0)
-
         mass_row = kept("mass_row", [1, V], F32)
         inv_row = kept("inv_row", [1, V], F32)
-        nc.scalar.dma_start(mass_row[:], mass[0:1, :])
-        nc.scalar.dma_start(inv_row[:], inv[0:1, :])
+        xs_table = kept("xs_table", [P, T], U8)
+        es_table = kept("es_table", [P, W], U8)
+        qn_table = kept("qn_table", [P, W], F32)
+        c_rows = kept("c_rows", [P, V], F32)
+        own_rows = kept("own_rows", [P, P], F32)
         ident = kept("ident", [P, P], F32)
+        w_raw = [kept("w_raw%d" % g, [P, PACK, H], F32) for g in range(PASSES)]
+        x_table = [kept("x_table%d" % g, [P, T], U32) for g in range(PASSES)]
+        e_table = kept("e_table", [P, W], U32)
+
+        nc.vector.memset(xs_table[:].bitcast(I32), 0)
+        nc.vector.memset(es_table[:].bitcast(I32), 0)
+        nc.vector.memset(c_rows[:], 0.0)
+        nc.vector.memset(own_rows[:], 0.0)
+        nc.gpsimd.memset(qn_table[:], 0.0)
         make_identity(nc, ident[:])
-        for q in range(4):
-            nc.scalar.dma_start(
-                xs_table[32 * q : 32 * q + 4 * PASSES, :].bitcast(I32),
-                x_scales[:, 4 * q : 4 * q + 4, :].bitcast(I32),
-            )
-        nc.gpsimd.dma_start(qn_table[0:1, :], qn[0:1, :])
-        nc.gpsimd.dma_start(rows[1 : 1 + TILES, 0:P], own.rearrange("(a m) o -> a (m o)", m=P))
-        for q in range(4):
-            nc.gpsimd.dma_start(
-                es_table[32 * q : 32 * q + 4, :].bitcast(I32), e_scales[0, 4 * q : 4 * q + 4, :].bitcast(I32)
-            )
+
+        def load_w(g):
+            nc.sync.dma_start(w_raw[g][:], w1[g * K_PASS : (g + 1) * K_PASS, :].rearrange("(p j) c -> p j c", j=PACK))
+
+        def load_words(table, words):
+            nc.sync.dma_start(table[:].bitcast(I32), words.rearrange("p n t -> p (n t)").bitcast(I32))
+
+        def load_scales(table, scales):
+            rows_q = 4 * scales.shape[0]
+            for q in range(4):
+                nc.sync.dma_start(
+                    table[32 * q : 32 * q + rows_q, :].bitcast(I32), scales[:, 4 * q : 4 * q + 4, :].bitcast(I32)
+                )
+
+        nc.sync.dma_start(mass_row[:], mass[0:1, :])
+        nc.sync.dma_start(inv_row[:], inv[0:1, :])
+        nc.sync.dma_start(offs_sb[:], offs)
+        load_w(0)
+        load_scales(xs_table, x_scales)
+        load_w(1)
+        nc.sync.dma_start(cen_sb[:], cen)
+        nc.sync.dma_start(qn_table[0:1, :], qn[0:1, :])
+        load_scales(es_table, e_scales)
+        load_words(x_table[0], x_words[0])
+        nc.sync.dma_start(own_rows[0:TILES, :], own.rearrange("(a m) o -> a (m o)", m=P))
+        load_words(x_table[1], x_words[1])
+        load_words(e_table, e_words[0])
 
         mass_sum = kept("mass_sum", [1, 1], F32)
         nc.vector.tensor_reduce(mass_sum[:], mass_row[:], AXIS.X, ALU.add, apply_absolute_value=True)
@@ -84,19 +92,20 @@ def tile_picked_ydec_tgt_p_kernel(
         nc.vector.tensor_scalar(share[:], mass_row[:], mass_root[:], mass_root[:], ALU.mult, ALU.mult)
         share_inv = kept("share_inv", [1, V], F32)
         nc.vector.tensor_tensor(share_inv[:], share[:], inv_row[:], ALU.mult)
-        nc.vector.tensor_tensor(rows[0:1, :], share_inv[:], share[:], ALU.mult)
+        nc.vector.tensor_tensor(c_rows[0:1, :], share_inv[:], share[:], ALU.mult)
 
-        w_codes = [kept("w_codes%d" % g, [P, H], U32) for g in range(PASSES)]
-        w_scales = [kept("w_scales%d" % g, [P, H], U8) for g in range(PASSES)]
+        w_codes = []
+        w_scales = []
         w_bf = [kept("w_bf%d" % g, [P, PACK * H], BF16) for g in range(PASSES)]
 
         def round_w(g):
             dst = w_bf[g][:].rearrange("p (t m j) -> p m t j", t=PACK, j=PACK)
             src = w_raw[g][:].rearrange("p j (m t) -> p m t j", t=PACK)
-            nc.scalar.copy(dst[:, 0:M_SCALAR], src[:, 0:M_SCALAR])
-            nc.vector.tensor_copy(dst[:, M_SCALAR:P], src[:, M_SCALAR:P])
+            nc.scalar.copy(dst, src)
 
-        def quantize_w(g):
+        def quantize_w(g, codes_tag, scales_tag):
+            w_codes.append(kept("w_codes%d" % g, [P, H], U32, tag=codes_tag))
+            w_scales.append(kept("w_scales%d" % g, [P, H], U8, tag=scales_tag))
             nc.vector.quantize_mx(out=w_codes[g][:].bitcast(FP8X4), scales=w_scales[g][:], in_=w_bf[g][:])
 
         xs_pick = kept("xs_pick", [P, S], U8)
@@ -105,33 +114,33 @@ def tile_picked_ydec_tgt_p_kernel(
         e_pick = kept("e_pick", [P, V], U32)
 
         round_w(0)
-        e_table = kept("e_table", [P, W], U32, tag="w_raw0")
-        nc.sync.dma_start(e_table[:].bitcast(I32), e_words[0].rearrange("p n t -> p (n t)").bitcast(I32))
-        nc.vector.tensor_copy(qn_pick[:], qn_table[:].indirect(cen_sb[:]))
-        nc.vector.tensor_copy(xs_pick[:], xs_table[:].indirect(offs_sb[:]))
-        quantize_w(0)
         round_w(1)
+        nc.vector.tensor_copy(xs_pick[:], xs_table[:].indirect(offs_sb[:]))
+        quantize_w(0, "xs_table", None)
+        nc.vector.tensor_copy(qn_pick[:], qn_table[:].indirect(cen_sb[:]))
         nc.vector.tensor_copy(es_pick[:], es_table[:].indirect(cen_sb[:]))
 
         turn = psum.tile([P, 4, P], F32, name="turn", tag="y")
         for b in range(2):
             nc.tensor.transpose(turn[:, b, :], qn_pick[:, b * P : (b + 1) * P], ident[:])
-            nc.tensor.transpose(turn[:, 2 + b, :], rows[:, b * P : (b + 1) * P], ident[:])
-        cols = kept("cols", [P, 4], F32, tag="es_table")
-        nc.vector.tensor_copy(cols[:], turn[:, :, 0])
-        own1 = kept("own1", [P, TILES], F32)
-        nc.vector.tensor_scalar_add(own1[:], turn[:, 2, 1 : 1 + TILES], 1.0)
+            nc.tensor.transpose(turn[:, 2 + b, :], c_rows[:, b * P : (b + 1) * P], ident[:])
+        cols = kept("cols", [P, 4], F32, tag="w_raw1")
+        nc.scalar.copy(cols[:], turn[:, :, 0])
         spread = psum.tile([P, 4, P], F32, name="spread", tag="y")
         for b in range(4):
             nc.tensor.transpose(spread[:, b, :], cols[:, b : b + 1].to_broadcast([P, P]), ident[:])
-        wide = kept("wide", [P, 2 * V], F32)
-        nc.vector.tensor_copy(wide[:], spread[:].rearrange("p b n -> p (b n)"))
+        wide = kept("wide", [P, 2 * V], F32, tag="w_raw1")
+        nc.scalar.copy(wide[:], spread[:].rearrange("p b n -> p (b n)"))
         qn_wide = wide[:, 0:V]
         c_wide = wide[:, V : 2 * V]
+        own_turn = psum.tile([P, 4, P], F32, name="own_turn", tag="y")
+        nc.tensor.transpose(own_turn[:, 0, :], own_rows[:], ident[:])
+        own1 = kept("own1", [P, TILES], F32)
+        nc.scalar.activation(own1[:], own_turn[:, 0, 0:TILES], ACT.Copy, bias=1.0)
 
-        quantize_w(1)
-        x_first = kept("x_first", [P, S], U32, tag="xs_table")
+        x_first = kept("x_first", [P, S], U32)
         nc.vector.tensor_copy(x_first[:], x_table[0][:].indirect(offs_sb[:]))
+        quantize_w(1, "qn_table", "es_table")
         h_banks = [psum.tile([P, PACK, P], F32, name="h", tag="h") for a in range(TILES)]
 
         def h_pass(a, j, g):
@@ -149,7 +158,7 @@ def tile_picked_ydec_tgt_p_kernel(
 
         for a in range(TILES):
             h_pass(a, 0, 0)
-        x_last = [kept("x_last0", [P, 256], U32, tag="es_table"), kept("x_last1", [P, 256], U32)]
+        x_last = [kept("x_last0", [P, 256], U32), kept("x_last1", [P, 256], U32)]
         for half in range(2):
             nc.vector.tensor_copy(x_last[half][:], x_table[1][:].indirect(offs_sb[:, half * 16 : (half + 1) * 16]))
         nc.vector.tensor_copy(e_pick[:], e_table[:].indirect(cen_sb[:]))

@@ -22,6 +22,7 @@ PACK = 4
 K_PASS = P * PACK
 PASSES = K // K_PASS
 TILES = S // P
+M_SCALAR = 88
 
 
 def tile_picked_ydec_tgt_p_kernel(
@@ -101,7 +102,8 @@ def tile_picked_ydec_tgt_p_kernel(
         def round_w(g):
             dst = w_bf[g][:].rearrange("p (t m j) -> p m t j", t=PACK, j=PACK)
             src = w_raw[g][:].rearrange("p j (m t) -> p m t j", t=PACK)
-            nc.scalar.copy(dst, src)
+            nc.scalar.copy(dst[:, 0:M_SCALAR], src[:, 0:M_SCALAR])
+            nc.vector.tensor_copy(dst[:, M_SCALAR:P], src[:, M_SCALAR:P])
 
         def quantize_w(g, codes_tag, scales_tag):
             w_codes.append(kept("w_codes%d" % g, [P, H], U32, tag=codes_tag))
@@ -141,6 +143,17 @@ def tile_picked_ydec_tgt_p_kernel(
         x_first = kept("x_first", [P, S], U32)
         nc.vector.tensor_copy(x_first[:], x_table[0][:].indirect(offs_sb[:]))
         quantize_w(1, "qn_table", "es_table")
+        for n in range(2):
+            warm = psum.tile([P, H], F32, name="warm", tag="y")
+            nc.tensor.matmul_mx(
+                out=warm[:],
+                lhsT=w_codes[0][:, 0:P].bitcast(FP8X4),
+                lhsT_scale=w_scales[0][:, 0:P],
+                rhs=w_codes[1][:].bitcast(FP8X4),
+                rhs_scale=w_scales[1][:],
+                start=True,
+                stop=True,
+            )
         h_banks = [psum.tile([P, PACK, P], F32, name="h", tag="h") for a in range(TILES)]
 
         def h_pass(a, j, g):

@@ -22,7 +22,8 @@ PACK = 4
 K_PASS = P * PACK
 PASSES = K // K_PASS
 TILES = S // P
-M_SCALAR = 88
+HALF = S // 2
+M_SCALAR = (104, 48)
 
 
 def tile_picked_ydec_tgt_p_kernel(
@@ -33,6 +34,7 @@ def tile_picked_ydec_tgt_p_kernel(
         keep = ctx.enter_context(tc.tile_pool(name="keep", bufs=1))
         work = ctx.enter_context(tc.tile_pool(name="work", bufs=4))
         psum = ctx.enter_context(tc.psum_pool(name="psum", bufs=4))
+        banks = ctx.enter_context(tc.psum_pool(name="banks", bufs=4))
 
         def kept(name, shape, dtype, tag=None):
             return keep.tile(shape, dtype, name=name, tag=tag or name, align_bytes=64)
@@ -41,11 +43,11 @@ def tile_picked_ydec_tgt_p_kernel(
         cen_sb = kept("cen_sb", [P, V // 16], U16)
         mass_row = kept("mass_row", [1, V], F32)
         inv_row = kept("inv_row", [1, V], F32)
+        own_rows = kept("own_rows", [P, P], F32)
         xs_table = kept("xs_table", [P, T], U8)
         es_table = kept("es_table", [P, W], U8)
         qn_table = kept("qn_table", [P, W], F32)
         c_rows = kept("c_rows", [P, V], F32)
-        own_rows = kept("own_rows", [P, P], F32)
         ident = kept("ident", [P, P], F32)
         w_raw = [kept("w_raw%d" % g, [P, PACK, H], F32) for g in range(PASSES)]
         x_table = [kept("x_table%d" % g, [P, T], U32) for g in range(PASSES)]
@@ -53,9 +55,9 @@ def tile_picked_ydec_tgt_p_kernel(
 
         nc.vector.memset(xs_table[:].bitcast(I32), 0)
         nc.vector.memset(es_table[:].bitcast(I32), 0)
+        nc.vector.memset(own_rows[0 : P - TILES, :], 0.0)
         nc.vector.memset(c_rows[:], 0.0)
-        nc.vector.memset(own_rows[:], 0.0)
-        nc.gpsimd.memset(qn_table[:], 0.0)
+        nc.gpsimd.memset(qn_table[0 : P - 1, :], 0.0)
         make_identity(nc, ident[:])
 
         def load_w(g):
@@ -71,17 +73,17 @@ def tile_picked_ydec_tgt_p_kernel(
                     table[32 * q : 32 * q + rows_q, :].bitcast(I32), scales[:, 4 * q : 4 * q + 4, :].bitcast(I32)
                 )
 
+        nc.sync.dma_start(cen_sb[:], cen)
+        nc.sync.dma_start(qn_table[P - 1 : P, :], qn[0:1, :])
         nc.sync.dma_start(mass_row[:], mass[0:1, :])
         nc.sync.dma_start(inv_row[:], inv[0:1, :])
-        nc.sync.dma_start(offs_sb[:], offs)
+        nc.sync.dma_start(own_rows[P - TILES : P, :], own.rearrange("(a m) o -> a (m o)", m=P))
         load_w(0)
+        nc.sync.dma_start(offs_sb[:], offs)
         load_scales(xs_table, x_scales)
         load_w(1)
-        nc.sync.dma_start(cen_sb[:], cen)
-        nc.sync.dma_start(qn_table[0:1, :], qn[0:1, :])
-        load_scales(es_table, e_scales)
         load_words(x_table[0], x_words[0])
-        nc.sync.dma_start(own_rows[0:TILES, :], own.rearrange("(a m) o -> a (m o)", m=P))
+        load_scales(es_table, e_scales)
         load_words(x_table[1], x_words[1])
         load_words(e_table, e_words[0])
 
@@ -89,8 +91,11 @@ def tile_picked_ydec_tgt_p_kernel(
         nc.vector.tensor_reduce(mass_sum[:], mass_row[:], AXIS.X, ALU.add, apply_absolute_value=True)
         mass_root = kept("mass_root", [1, 1], F32)
         nc.scalar.activation(mass_root[:], mass_sum[:], ACT.Abs_reciprocal_sqrt)
+        qn_pick = kept("qn_pick", [P, V], F32)
+        nc.vector.tensor_copy(qn_pick[:], qn_table[:].indirect(cen_sb[:]))
         share = kept("share", [1, V], F32)
         nc.vector.tensor_scalar(share[:], mass_row[:], mass_root[:], mass_root[:], ALU.mult, ALU.mult)
+
         share_inv = kept("share_inv", [1, V], F32)
         nc.vector.tensor_tensor(share_inv[:], share[:], inv_row[:], ALU.mult)
         nc.vector.tensor_tensor(c_rows[0:1, :], share_inv[:], share[:], ALU.mult)
@@ -102,78 +107,92 @@ def tile_picked_ydec_tgt_p_kernel(
         def round_w(g):
             dst = w_bf[g][:].rearrange("p (t m j) -> p m t j", t=PACK, j=PACK)
             src = w_raw[g][:].rearrange("p j (m t) -> p m t j", t=PACK)
-            nc.scalar.copy(dst[:, 0:M_SCALAR], src[:, 0:M_SCALAR])
-            nc.vector.tensor_copy(dst[:, M_SCALAR:P], src[:, M_SCALAR:P])
+            nc.scalar.copy(dst[:, 0 : M_SCALAR[g]], src[:, 0 : M_SCALAR[g]])
+            nc.vector.tensor_copy(dst[:, M_SCALAR[g] : P], src[:, M_SCALAR[g] : P])
 
         def quantize_w(g, codes_tag, scales_tag):
             w_codes.append(kept("w_codes%d" % g, [P, H], U32, tag=codes_tag))
             w_scales.append(kept("w_scales%d" % g, [P, H], U8, tag=scales_tag))
             nc.vector.quantize_mx(out=w_codes[g][:].bitcast(FP8X4), scales=w_scales[g][:], in_=w_bf[g][:])
 
-        xs_pick = kept("xs_pick", [P, S], U8)
+        xs_pick = kept("xs_pick", [P, S], U8, tag="share_inv")
         es_pick = kept("es_pick", [P, V], U8)
-        qn_pick = kept("qn_pick", [P, V], F32)
-        e_pick = kept("e_pick", [P, V], U32)
 
         round_w(0)
-        round_w(1)
         nc.vector.tensor_copy(xs_pick[:], xs_table[:].indirect(offs_sb[:]))
         quantize_w(0, "xs_table", None)
-        nc.vector.tensor_copy(qn_pick[:], qn_table[:].indirect(cen_sb[:]))
-        nc.vector.tensor_copy(es_pick[:], es_table[:].indirect(cen_sb[:]))
+        round_w(1)
+        quantize_w(1, None, None)
 
-        turn = psum.tile([P, 4, P], F32, name="turn", tag="y")
+        turn = psum.tile([P, 3, P], F32, name="turn", tag="y")
+        nc.tensor.transpose(turn[:, 2, :], own_rows[:], ident[:])
         for b in range(2):
             nc.tensor.transpose(turn[:, b, :], qn_pick[:, b * P : (b + 1) * P], ident[:])
-            nc.tensor.transpose(turn[:, 2 + b, :], c_rows[:, b * P : (b + 1) * P], ident[:])
-        cols = kept("cols", [P, 4], F32, tag="w_raw1")
-        nc.scalar.copy(cols[:], turn[:, :, 0])
+        small = kept("small", [P, 13], F32, tag="w_raw1")
+        qn_cols, c_cols, own1, own_abs, own_sum = (small[:, 0:2], small[:, 2:4], small[:, 4:8], small[:, 8:12], small[:, 12:13])
+        nc.scalar.copy(qn_cols, turn[:, 0:2, P - 1])
+        nc.scalar.activation(own1, turn[:, 2, P - TILES : P], ACT.Copy, bias=1.0)
+        nc.scalar.activation(own_abs, turn[:, 2, P - TILES : P], ACT.Abs, accum_out=own_sum)
+        c_turn = psum.tile([P, 2, P], F32, name="c_turn", tag="y")
+        for b in range(2):
+            nc.tensor.transpose(c_turn[:, b, :], c_rows[:, b * P : (b + 1) * P], ident[:])
+        nc.scalar.copy(c_cols, c_turn[:, :, 0])
         spread = psum.tile([P, 4, P], F32, name="spread", tag="y")
         for b in range(4):
-            nc.tensor.transpose(spread[:, b, :], cols[:, b : b + 1].to_broadcast([P, P]), ident[:])
-        wide = kept("wide", [P, 2 * V], F32, tag="w_raw1")
+            nc.tensor.transpose(spread[:, b, :], small[:, b : b + 1].to_broadcast([P, P]), ident[:])
+        wide = kept("wide", [P, 2 * V], F32)
         nc.scalar.copy(wide[:], spread[:].rearrange("p b n -> p (b n)"))
         qn_wide = wide[:, 0:V]
         c_wide = wide[:, V : 2 * V]
-        own_turn = psum.tile([P, 4, P], F32, name="own_turn", tag="y")
-        nc.tensor.transpose(own_turn[:, 0, :], own_rows[:], ident[:])
-        own1 = kept("own1", [P, TILES], F32)
-        nc.scalar.activation(own1[:], own_turn[:, 0, 0:TILES], ACT.Copy, bias=1.0)
 
-        x_first = kept("x_first", [P, S], U32)
-        nc.vector.tensor_copy(x_first[:], x_table[0][:].indirect(offs_sb[:]))
-        quantize_w(1, "qn_table", "es_table")
-        for n in range(2):
-            warm = psum.tile([P, H], F32, name="warm", tag="y")
-            nc.tensor.matmul_mx(
-                out=warm[:],
-                lhsT=w_codes[0][:, 0:P].bitcast(FP8X4),
-                lhsT_scale=w_scales[0][:, 0:P],
-                rhs=w_codes[1][:].bitcast(FP8X4),
-                rhs_scale=w_scales[1][:],
-                start=True,
-                stop=True,
+        qn_abs = kept("qn_abs", [P, V], F32)
+        qn_mean = kept("qn_mean", [P, 1], F32)
+        nc.scalar.activation(qn_abs[:], qn_wide, ACT.Abs, scale=1.0 / V, accum_out=qn_mean[:])
+        size = kept("size", [P, 1], F32)
+        nc.scalar.activation(size[:], own_sum, ACT.Identity, bias=qn_mean[:])
+        alpha = kept("alpha", [P, 1], F32)
+        nc.scalar.activation(alpha[:], size[:], ACT.Abs_reciprocal_sqrt, bias=1.0)
+        beta = kept("beta", [P, TILES], F32)
+        nc.scalar.activation(beta[:], own1, ACT.Copy, scale=alpha[:])
+
+        h_banks = [banks.tile([P, PACK, P], F32, name="h", tag="h") for a in range(TILES)]
+        x_pick = [kept("x_pick0", [P, S], U32, tag="w_bf1"), kept("x_pick1", [P, S], U32, tag="x_table0")]
+
+        def gather_x(g, half):
+            nc.vector.tensor_copy(
+                x_pick[g][:, half * HALF : (half + 1) * HALF],
+                x_table[g][:].indirect(offs_sb[:, half * HALF // 16 : (half + 1) * HALF // 16]),
             )
-        h_banks = [psum.tile([P, PACK, P], F32, name="h", tag="h") for a in range(TILES)]
 
         def h_pass(a, j, g):
-            cols_a = slice(a * P, (a + 1) * P)
-            moving = x_first[:, cols_a] if g == 0 else x_last[a // 2][:, (a % 2) * P : (a % 2 + 1) * P]
             nc.tensor.matmul_mx(
                 out=h_banks[a][:, j, :],
                 lhsT=w_codes[g][:, j * P : (j + 1) * P].bitcast(FP8X4),
                 lhsT_scale=w_scales[g][:, j * P : (j + 1) * P],
-                rhs=moving.bitcast(FP8X4),
-                rhs_scale=xs_pick[4 * g : P, cols_a],
+                rhs=x_pick[g][:, a * P : (a + 1) * P].bitcast(FP8X4),
+                rhs_scale=xs_pick[4 * g : P, a * P : (a + 1) * P],
                 start=(g == 0),
                 stop=(g == PASSES - 1),
             )
 
-        for a in range(TILES):
-            h_pass(a, 0, 0)
-        x_last = [kept("x_last0", [P, 256], U32), kept("x_last1", [P, 256], U32)]
         for half in range(2):
-            nc.vector.tensor_copy(x_last[half][:], x_table[1][:].indirect(offs_sb[:, half * 16 : (half + 1) * 16]))
+            gather_x(0, half)
+            h_pass(2 * half, 0, 0)
+            h_pass(2 * half + 1, 0, 0)
+            warm = psum.tile([P, H], F32, name="warm", tag="y")
+            nc.tensor.matmul_mx(
+                out=warm[:],
+                lhsT=x_pick[0][:, half * HALF : half * HALF + P].bitcast(FP8X4),
+                lhsT_scale=xs_pick[:, 2 * half * P : (2 * half + 1) * P],
+                rhs=w_codes[0][:].bitcast(FP8X4),
+                rhs_scale=w_scales[0][:],
+                start=True,
+                stop=True,
+            )
+        nc.vector.tensor_copy(es_pick[:], es_table[:].indirect(cen_sb[:]))
+        for half in range(2):
+            gather_x(1, half)
+        e_pick = kept("e_pick", [P, V], U32, tag="x_table1")
         nc.vector.tensor_copy(e_pick[:], e_table[:].indirect(cen_sb[:]))
 
         state = [dict() for a in range(TILES)]
@@ -213,20 +232,19 @@ def tile_picked_ydec_tgt_p_kernel(
             part = wt(a, "part", [P, V], F32)
             nc.vector.scalar_tensor_tensor(part[:], state[a]["y"][:, 0:V], -0.2, qn_wide, ALU.mult, ALU.add)
             root = wt(a, "root", [P, V], F32)
-            nc.scalar.activation(root[:], part[:], ACT.Abs_reciprocal_sqrt, bias=own1[:, a : a + 1])
+            nc.scalar.activation(
+                root[:], part[:], ACT.Abs_reciprocal_sqrt, bias=beta[:, a : a + 1], scale=alpha[:]
+            )
             kern = wt(a, "kern", [P, V], F32)
-            kern_sum = wt(a, "kern_sum", [P, 1], F32)
-            nc.scalar.activation(kern[:], root[:], ACT.Square, accum_out=kern_sum[:])
+            nc.scalar.activation(kern[:], root[:], ACT.Square)
 
         def weigh(a):
             kern = state[a]["kern"]
-            norm = wt(a, "norm", [P, 1], F32)
-            nc.vector.reciprocal(norm[:], state[a]["kern_sum"][:])
-            left = wt(a, "left", [P, V], F32)
-            nc.vector.tensor_tensor(left[:], kern[:], c_wide, ALU.mult)
             rr = wt(a, "rr", [P, V], F32)
             rr_sum = wt(a, "rr_sum", [P, 1], F32)
-            nc.vector.scalar_tensor_tensor(rr[:], kern[:], norm[:], left[:], ALU.mult, ALU.mult, accum_out=rr_sum[:])
+            left = wt(a, "left", [P, V], F32)
+            nc.vector.tensor_tensor(left[:], c_wide, kern[:], ALU.mult)
+            nc.vector.scalar_tensor_tensor(rr[:], kern[:], 1.0, left[:], ALU.mult, ALU.mult, accum_out=rr_sum[:])
 
         def finish(a):
             norm2 = wt(a, "norm2", [P, 1], F32)

@@ -23,7 +23,7 @@ K_PASS = P * PACK
 PASSES = K // K_PASS
 TILES = S // P
 HALF = S // 2
-M_SCALAR = (104, 48)
+M_SCALAR = (48, 72)
 
 
 def tile_picked_ydec_tgt_p_kernel(
@@ -74,14 +74,14 @@ def tile_picked_ydec_tgt_p_kernel(
                 )
 
         nc.sync.dma_start(cen_sb[:], cen)
-        nc.sync.dma_start(qn_table[P - 1 : P, :], qn[0:1, :])
-        nc.sync.dma_start(mass_row[:], mass[0:1, :])
-        nc.sync.dma_start(inv_row[:], inv[0:1, :])
-        nc.sync.dma_start(own_rows[P - TILES : P, :], own.rearrange("(a m) o -> a (m o)", m=P))
         load_w(0)
+        nc.scalar.dma_start(qn_table[P - 1 : P, :], qn[0:1, :])
+        nc.scalar.dma_start(mass_row[:], mass[0:1, :])
+        nc.scalar.dma_start(inv_row[:], inv[0:1, :])
+        nc.scalar.dma_start(own_rows[P - TILES : P, :], own.rearrange("(a m) o -> a (m o)", m=P))
         nc.sync.dma_start(offs_sb[:], offs)
-        load_scales(xs_table, x_scales)
         load_w(1)
+        load_scales(xs_table, x_scales)
         load_words(x_table[0], x_words[0])
         load_scales(es_table, e_scales)
         load_words(x_table[1], x_words[1])
@@ -115,14 +115,14 @@ def tile_picked_ydec_tgt_p_kernel(
             w_scales.append(kept("w_scales%d" % g, [P, H], U8, tag=scales_tag))
             nc.vector.quantize_mx(out=w_codes[g][:].bitcast(FP8X4), scales=w_scales[g][:], in_=w_bf[g][:])
 
-        xs_pick = kept("xs_pick", [P, S], U8, tag="share_inv")
+        xs_pick = kept("xs_pick", [P, S], U8, tag="w_bf0")
         es_pick = kept("es_pick", [P, V], U8)
 
         round_w(0)
-        nc.vector.tensor_copy(xs_pick[:], xs_table[:].indirect(offs_sb[:]))
-        quantize_w(0, "xs_table", None)
+        quantize_w(0, None, None)
         round_w(1)
-        quantize_w(1, None, None)
+        nc.vector.tensor_copy(xs_pick[:], xs_table[:].indirect(offs_sb[:]))
+        quantize_w(1, "xs_table", None)
 
         turn = psum.tile([P, 3, P], F32, name="turn", tag="y")
         nc.tensor.transpose(turn[:, 2, :], own_rows[:], ident[:])

@@ -33,6 +33,7 @@ def tile_picked_ydec_tgt_p_kernel(
     with ExitStack() as ctx:
         keep = ctx.enter_context(tc.tile_pool(name="keep", bufs=1))
         work = ctx.enter_context(tc.tile_pool(name="work", bufs=4))
+        pair = ctx.enter_context(tc.tile_pool(name="pair", bufs=2))
         psum = ctx.enter_context(tc.psum_pool(name="psum", bufs=4))
         banks = ctx.enter_context(tc.psum_pool(name="banks", bufs=4))
 
@@ -68,7 +69,7 @@ def tile_picked_ydec_tgt_p_kernel(
 
         def load_scales(table, scales):
             rows_q = 4 * scales.shape[0]
-            for q in range(4):
+            for q in (0, 2, 1, 3):
                 nc.sync.dma_start(
                     table[32 * q : 32 * q + rows_q, :].bitcast(I32), scales[:, 4 * q : 4 * q + 4, :].bitcast(I32)
                 )
@@ -83,8 +84,8 @@ def tile_picked_ydec_tgt_p_kernel(
         load_w(1)
         load_scales(xs_table, x_scales)
         load_words(x_table[0], x_words[0])
-        load_scales(es_table, e_scales)
         load_words(x_table[1], x_words[1])
+        load_scales(es_table, e_scales)
         load_words(e_table, e_words[0])
 
         mass_sum = kept("mass_sum", [1, 1], F32)
@@ -116,7 +117,6 @@ def tile_picked_ydec_tgt_p_kernel(
             nc.vector.quantize_mx(out=w_codes[g][:].bitcast(FP8X4), scales=w_scales[g][:], in_=w_bf[g][:])
 
         xs_pick = kept("xs_pick", [P, S], U8, tag="w_bf0")
-        es_pick = kept("es_pick", [P, V], U8)
 
         round_w(0)
         quantize_w(0, None, None)
@@ -189,10 +189,11 @@ def tile_picked_ydec_tgt_p_kernel(
                 start=True,
                 stop=True,
             )
-        nc.vector.tensor_copy(es_pick[:], es_table[:].indirect(cen_sb[:]))
         for half in range(2):
             gather_x(1, half)
-        e_pick = kept("e_pick", [P, V], U32, tag="x_table1")
+        es_pick = kept("es_pick", [P, V], U8, tag="x_table1")
+        nc.vector.tensor_copy(es_pick[:], es_table[:].indirect(cen_sb[:]))
+        e_pick = kept("e_pick", [P, V], U32, tag="es_table")
         nc.vector.tensor_copy(e_pick[:], e_table[:].indirect(cen_sb[:]))
 
         state = [dict() for a in range(TILES)]
@@ -211,7 +212,7 @@ def tile_picked_ydec_tgt_p_kernel(
             nc.scalar.copy(h_bf[:], h[:].rearrange("p j n -> p n j"))
 
         def inner(a):
-            h_codes = wt(a, "h_codes", [P, P], U32)
+            h_codes = kept("h_codes%d" % a, [P, P], U32, tag="h_codes_odd" if a % 2 else "e_table")
             h_scales = wt(a, "h_scales", [P, P], U8)
             nc.vector.quantize_mx(
                 out=h_codes[:].bitcast(FP8X4), scales=h_scales[:], in_=state[a]["h_bf"][:].rearrange("p n j -> p (n j)")
@@ -231,7 +232,7 @@ def tile_picked_ydec_tgt_p_kernel(
         def distance(a):
             part = wt(a, "part", [P, V], F32)
             nc.vector.scalar_tensor_tensor(part[:], state[a]["y"][:, 0:V], -0.2, qn_wide, ALU.mult, ALU.add)
-            root = wt(a, "root", [P, V], F32)
+            root = pair.tile([P, V], F32, name="root", align_bytes=64)
             nc.scalar.activation(
                 root[:], part[:], ACT.Abs_reciprocal_sqrt, bias=beta[:, a : a + 1], scale=alpha[:]
             )

@@ -23,7 +23,7 @@ K_PASS = P * PACK
 PASSES = K // K_PASS
 TILES = S // P
 HALF = S // 2
-M_SCALAR = (48, 72)
+M_SCALAR = (48, 48)
 
 
 def tile_picked_ydec_tgt_p_kernel(
@@ -67,12 +67,11 @@ def tile_picked_ydec_tgt_p_kernel(
         def load_words(table, words):
             nc.sync.dma_start(table[:].bitcast(I32), words.rearrange("p n t -> p (n t)").bitcast(I32))
 
-        def load_scales(table, scales):
-            rows_q = 4 * scales.shape[0]
-            for q in (0, 2, 1, 3):
-                nc.sync.dma_start(
-                    table[32 * q : 32 * q + rows_q, :].bitcast(I32), scales[:, 4 * q : 4 * q + 4, :].bitcast(I32)
-                )
+        def load_scales(table, scales, quadrants):
+            for q in quadrants:
+                for g in range(scales.shape[0]):
+                    row = 32 * q + 4 * g
+                    nc.sync.dma_start(table[row : row + 4, :].bitcast(I32), scales[g, 4 * q : 4 * q + 4, :].bitcast(I32))
 
         nc.sync.dma_start(cen_sb[:], cen)
         load_w(0)
@@ -82,10 +81,11 @@ def tile_picked_ydec_tgt_p_kernel(
         nc.scalar.dma_start(own_rows[P - TILES : P, :], own.rearrange("(a m) o -> a (m o)", m=P))
         nc.sync.dma_start(offs_sb[:], offs)
         load_w(1)
-        load_scales(xs_table, x_scales)
+        load_scales(xs_table, x_scales, (0, 2))
         load_words(x_table[0], x_words[0])
+        load_scales(xs_table, x_scales, (1, 3))
         load_words(x_table[1], x_words[1])
-        load_scales(es_table, e_scales)
+        load_scales(es_table, e_scales, (0, 2, 1, 3))
         load_words(e_table, e_words[0])
 
         mass_sum = kept("mass_sum", [1, 1], F32)
@@ -116,13 +116,11 @@ def tile_picked_ydec_tgt_p_kernel(
             w_scales.append(kept("w_scales%d" % g, [P, H], U8, tag=scales_tag))
             nc.vector.quantize_mx(out=w_codes[g][:].bitcast(FP8X4), scales=w_scales[g][:], in_=w_bf[g][:])
 
-        xs_pick = kept("xs_pick", [P, S], U8, tag="w_bf0")
 
         round_w(0)
         quantize_w(0, None, None)
         round_w(1)
-        nc.vector.tensor_copy(xs_pick[:], xs_table[:].indirect(offs_sb[:]))
-        quantize_w(1, "xs_table", None)
+        quantize_w(1, None, None)
 
         turn = psum.tile([P, 3, P], F32, name="turn", tag="y")
         nc.tensor.transpose(turn[:, 2, :], own_rows[:], ident[:])
@@ -156,7 +154,7 @@ def tile_picked_ydec_tgt_p_kernel(
         nc.scalar.activation(beta[:], own1, ACT.Copy, scale=alpha[:])
 
         h_banks = [banks.tile([P, PACK, P], F32, name="h", tag="h") for a in range(TILES)]
-        x_pick = [kept("x_pick0", [P, S], U32, tag="w_bf1"), kept("x_pick1", [P, S], U32, tag="x_table0")]
+        x_pick = [kept("x_pick0", [P, S], U32, tag="w_bf1"), kept("x_pick1", [P, S], U32, tag="xs_table")]
 
         def gather_x(g, half):
             nc.vector.tensor_copy(
@@ -177,18 +175,20 @@ def tile_picked_ydec_tgt_p_kernel(
 
         for half in range(2):
             gather_x(0, half)
-            h_pass(2 * half, 0, 0)
-            h_pass(2 * half + 1, 0, 0)
             warm = psum.tile([P, H], F32, name="warm", tag="y")
             nc.tensor.matmul_mx(
                 out=warm[:],
                 lhsT=x_pick[0][:, half * HALF : half * HALF + P].bitcast(FP8X4),
-                lhsT_scale=xs_pick[:, 2 * half * P : (2 * half + 1) * P],
+                lhsT_scale=w_scales[0][:, 0:P],
                 rhs=w_codes[0][:].bitcast(FP8X4),
                 rhs_scale=w_scales[0][:],
                 start=True,
                 stop=True,
             )
+        xs_pick = kept("xs_pick", [P, S], U8, tag="x_table0")
+        nc.vector.tensor_copy(xs_pick[:], xs_table[:].indirect(offs_sb[:]))
+        for a in range(TILES):
+            h_pass(a, 0, 0)
         for half in range(2):
             gather_x(1, half)
         es_pick = kept("es_pick", [P, V], U8, tag="x_table1")

@@ -23,7 +23,11 @@ K_PASS = P * PACK
 PASSES = K // K_PASS
 TILES = S // P
 HALF = S // 2
-M_SCALAR = (48, 48)
+GROUP = 16
+SCALE_ROWS = 4
+V_BLOCKS = V // P
+LAST = P - 1
+ROUND_ON_SCALAR = (80, 48)
 
 
 def tile_picked_ydec_tgt_p_kernel(
@@ -32,16 +36,16 @@ def tile_picked_ydec_tgt_p_kernel(
     nc = tc.nc
     with ExitStack() as ctx:
         keep = ctx.enter_context(tc.tile_pool(name="keep", bufs=1))
-        work = ctx.enter_context(tc.tile_pool(name="work", bufs=4))
+        work = ctx.enter_context(tc.tile_pool(name="work", bufs=TILES))
         pair = ctx.enter_context(tc.tile_pool(name="pair", bufs=2))
         psum = ctx.enter_context(tc.psum_pool(name="psum", bufs=4))
-        banks = ctx.enter_context(tc.psum_pool(name="banks", bufs=4))
+        banks = ctx.enter_context(tc.psum_pool(name="banks", bufs=TILES))
 
         def kept(name, shape, dtype, tag=None):
             return keep.tile(shape, dtype, name=name, tag=tag or name, align_bytes=64)
 
-        offs_sb = kept("offs_sb", [P, S // 16], U16)
-        cen_sb = kept("cen_sb", [P, V // 16], U16)
+        offs_sb = kept("offs_sb", [P, S // GROUP], U16)
+        cen_sb = kept("cen_sb", [P, V // GROUP], U16)
         mass_row = kept("mass_row", [1, V], F32)
         inv_row = kept("inv_row", [1, V], F32)
         own_rows = kept("own_rows", [P, P], F32)
@@ -58,7 +62,7 @@ def tile_picked_ydec_tgt_p_kernel(
         nc.vector.memset(es_table[:].bitcast(I32), 0)
         nc.vector.memset(own_rows[0 : P - TILES, :], 0.0)
         nc.vector.memset(c_rows[:], 0.0)
-        nc.gpsimd.memset(qn_table[0 : P - 1, :], 0.0)
+        nc.gpsimd.memset(qn_table[0:LAST, :], 0.0)
         make_identity(nc, ident[:])
 
         def load_w(g):
@@ -67,25 +71,30 @@ def tile_picked_ydec_tgt_p_kernel(
         def load_words(table, words):
             nc.sync.dma_start(table[:].bitcast(I32), words.rearrange("p n t -> p (n t)").bitcast(I32))
 
-        def load_scales(table, scales, quadrants):
-            for q in quadrants:
-                for g in range(scales.shape[0]):
-                    row = 32 * q + 4 * g
-                    nc.sync.dma_start(table[row : row + 4, :].bitcast(I32), scales[g, 4 * q : 4 * q + 4, :].bitcast(I32))
+        def load_scales(table, scales, q, first, count):
+            row = 32 * q + SCALE_ROWS * first
+            nc.sync.dma_start(
+                table[row : row + SCALE_ROWS * count, :].bitcast(I32),
+                scales[first : first + count, SCALE_ROWS * q : SCALE_ROWS * (q + 1), :].bitcast(I32),
+            )
 
         nc.sync.dma_start(cen_sb[:], cen)
         load_w(0)
-        nc.scalar.dma_start(qn_table[P - 1 : P, :], qn[0:1, :])
+        nc.scalar.dma_start(qn_table[LAST:P, :], qn[0:1, :])
         nc.scalar.dma_start(mass_row[:], mass[0:1, :])
         nc.scalar.dma_start(inv_row[:], inv[0:1, :])
-        nc.scalar.dma_start(own_rows[P - TILES : P, :], own.rearrange("(a m) o -> a (m o)", m=P))
+        nc.sync.dma_start(own_rows[P - TILES : P, :], own.rearrange("(a m) o -> a (m o)", m=P))
         nc.sync.dma_start(offs_sb[:], offs)
-        load_w(1)
-        load_scales(xs_table, x_scales, (0, 2))
         load_words(x_table[0], x_words[0])
-        load_scales(xs_table, x_scales, (1, 3))
+        for q in (0, 2):
+            for g in range(PASSES):
+                load_scales(xs_table, x_scales, q, g, 1)
+        for q in (1, 3):
+            load_scales(xs_table, x_scales, q, 0, PASSES)
+        load_w(1)
         load_words(x_table[1], x_words[1])
-        load_scales(es_table, e_scales, (0, 2, 1, 3))
+        for q in (0, 2, 1, 3):
+            load_scales(es_table, e_scales, q, 0, 1)
         load_words(e_table, e_words[0])
 
         mass_sum = kept("mass_sum", [1, 1], F32)
@@ -96,50 +105,64 @@ def tile_picked_ydec_tgt_p_kernel(
         nc.vector.tensor_copy(qn_pick[:], qn_table[:].indirect(cen_sb[:]))
         share = kept("share", [1, V], F32)
         nc.vector.tensor_scalar(share[:], mass_row[:], mass_root[:], mass_root[:], ALU.mult, ALU.mult)
-
         share_inv = kept("share_inv", [1, V], F32)
         nc.vector.tensor_tensor(share_inv[:], share[:], inv_row[:], ALU.mult)
         nc.vector.tensor_tensor(c_rows[0:1, :], share_inv[:], share[:], ALU.mult)
 
+        w_bf = []
         w_codes = []
         w_scales = []
-        w_bf = [kept("w_bf%d" % g, [P, PACK * H], BF16) for g in range(PASSES)]
 
-        def round_w(g):
+        def round_w(g, tag):
+            w_bf.append(kept("w_bf%d" % g, [P, PACK * H], BF16, tag=tag))
             dst = w_bf[g][:].rearrange("p (t m j) -> p m t j", t=PACK, j=PACK)
             src = w_raw[g][:].rearrange("p j (m t) -> p m t j", t=PACK)
-            nc.scalar.copy(dst[:, 0 : M_SCALAR[g]], src[:, 0 : M_SCALAR[g]])
-            nc.vector.tensor_copy(dst[:, M_SCALAR[g] : P], src[:, M_SCALAR[g] : P])
+            split = ROUND_ON_SCALAR[g]
+            nc.scalar.copy(dst[:, 0:split], src[:, 0:split])
+            nc.vector.tensor_copy(dst[:, split:P], src[:, split:P])
 
-        def quantize_w(g, codes_tag, scales_tag):
-            w_codes.append(kept("w_codes%d" % g, [P, H], U32, tag=codes_tag))
-            w_scales.append(kept("w_scales%d" % g, [P, H], U8, tag=scales_tag))
+        def quantize_w(g):
+            w_codes.append(kept("w_codes%d" % g, [P, H], U32))
+            w_scales.append(kept("w_scales%d" % g, [P, H], U8))
             nc.vector.quantize_mx(out=w_codes[g][:].bitcast(FP8X4), scales=w_scales[g][:], in_=w_bf[g][:])
 
+        round_w(0, None)
+        quantize_w(0)
+        x_first = kept("x_first", [P, S], U32, tag="w_bf0")
+        nc.vector.tensor_copy(x_first[:], x_table[0][:].indirect(offs_sb[:]))
 
-        round_w(0)
-        quantize_w(0, None, None)
-        round_w(1)
-        quantize_w(1, None, None)
-
-        turn = psum.tile([P, 3, P], F32, name="turn", tag="y")
-        nc.tensor.transpose(turn[:, 2, :], own_rows[:], ident[:])
-        for b in range(2):
+        turn = psum.tile([P, V_BLOCKS + 1, P], F32, name="turn", tag="y")
+        nc.tensor.transpose(turn[:, V_BLOCKS, :], own_rows[:], ident[:])
+        for b in range(V_BLOCKS):
             nc.tensor.transpose(turn[:, b, :], qn_pick[:, b * P : (b + 1) * P], ident[:])
-        small = kept("small", [P, 13], F32, tag="w_raw1")
-        qn_cols, c_cols, own1, own_abs, own_sum = (small[:, 0:2], small[:, 2:4], small[:, 4:8], small[:, 8:12], small[:, 12:13])
-        nc.scalar.copy(qn_cols, turn[:, 0:2, P - 1])
-        nc.scalar.activation(own1, turn[:, 2, P - TILES : P], ACT.Copy, bias=1.0)
-        nc.scalar.activation(own_abs, turn[:, 2, P - TILES : P], ACT.Abs, accum_out=own_sum)
-        c_turn = psum.tile([P, 2, P], F32, name="c_turn", tag="y")
-        for b in range(2):
+        own_cols = turn[:, V_BLOCKS, P - TILES : P]
+        cols = kept("cols", [P, 2 * V_BLOCKS + 2 * TILES + 1], F32, tag="w_raw0")
+        qn_cols = cols[:, 0:V_BLOCKS]
+        c_cols = cols[:, V_BLOCKS : 2 * V_BLOCKS]
+        own1 = cols[:, 2 * V_BLOCKS : 2 * V_BLOCKS + TILES]
+        own_abs = cols[:, 2 * V_BLOCKS + TILES : 2 * V_BLOCKS + 2 * TILES]
+        own_sum = cols[:, 2 * V_BLOCKS + 2 * TILES :]
+        nc.scalar.copy(qn_cols, turn[:, 0:V_BLOCKS, LAST])
+        nc.scalar.activation(own1, own_cols, ACT.Copy, bias=1.0)
+        nc.scalar.activation(own_abs, own_cols, ACT.Abs, accum_out=own_sum)
+        c_turn = psum.tile([P, V_BLOCKS, P], F32, name="c_turn", tag="y")
+        for b in range(V_BLOCKS):
             nc.tensor.transpose(c_turn[:, b, :], c_rows[:, b * P : (b + 1) * P], ident[:])
         nc.scalar.copy(c_cols, c_turn[:, :, 0])
-        spread = psum.tile([P, 4, P], F32, name="spread", tag="y")
-        for b in range(4):
-            nc.tensor.transpose(spread[:, b, :], small[:, b : b + 1].to_broadcast([P, P]), ident[:])
-        wide = kept("wide", [P, 2 * V], F32)
-        nc.scalar.copy(wide[:], spread[:].rearrange("p b n -> p (b n)"))
+        spread = [banks.tile([P, P], F32, name="spread", tag="h") for b in range(2 * V_BLOCKS)]
+        for b in range(2 * V_BLOCKS):
+            nc.tensor.transpose(spread[b][:], cols[:, b : b + 1].to_broadcast([P, P]), ident[:])
+
+        xs_pick = kept("xs_pick", [P, S], U8, tag="x_table0")
+        nc.vector.tensor_copy(xs_pick[:], xs_table[:].indirect(offs_sb[:]))
+        round_w(1, "xs_table")
+        quantize_w(1)
+        x_last = kept("x_last", [P, S], U32, tag="xs_table")
+        x_pick = (x_first, x_last)
+
+        wide = kept("wide", [P, 2 * V], F32, tag="w_raw1")
+        for b in range(2 * V_BLOCKS):
+            nc.scalar.copy(wide[:, b * P : (b + 1) * P], spread[b][:])
         qn_wide = wide[:, 0:V]
         c_wide = wide[:, V : 2 * V]
 
@@ -154,43 +177,24 @@ def tile_picked_ydec_tgt_p_kernel(
         nc.scalar.activation(beta[:], own1, ACT.Copy, scale=alpha[:])
 
         h_banks = [banks.tile([P, PACK, P], F32, name="h", tag="h") for a in range(TILES)]
-        x_pick = [kept("x_pick0", [P, S], U32, tag="w_bf1"), kept("x_pick1", [P, S], U32, tag="xs_table")]
 
-        def gather_x(g, half):
-            nc.vector.tensor_copy(
-                x_pick[g][:, half * HALF : (half + 1) * HALF],
-                x_table[g][:].indirect(offs_sb[:, half * HALF // 16 : (half + 1) * HALF // 16]),
-            )
-
-        def h_pass(a, j, g):
+        def h_pass(a, t, g):
             nc.tensor.matmul_mx(
-                out=h_banks[a][:, j, :],
-                lhsT=w_codes[g][:, j * P : (j + 1) * P].bitcast(FP8X4),
-                lhsT_scale=w_scales[g][:, j * P : (j + 1) * P],
+                out=h_banks[a][:, t, :],
+                lhsT=w_codes[g][:, t * P : (t + 1) * P].bitcast(FP8X4),
+                lhsT_scale=w_scales[g][:, t * P : (t + 1) * P],
                 rhs=x_pick[g][:, a * P : (a + 1) * P].bitcast(FP8X4),
-                rhs_scale=xs_pick[4 * g : P, a * P : (a + 1) * P],
+                rhs_scale=xs_pick[SCALE_ROWS * g : P, a * P : (a + 1) * P],
                 start=(g == 0),
                 stop=(g == PASSES - 1),
             )
 
-        for half in range(2):
-            gather_x(0, half)
-            warm = psum.tile([P, H], F32, name="warm", tag="y")
-            nc.tensor.matmul_mx(
-                out=warm[:],
-                lhsT=x_pick[0][:, half * HALF : half * HALF + P].bitcast(FP8X4),
-                lhsT_scale=w_scales[0][:, 0:P],
-                rhs=w_codes[0][:].bitcast(FP8X4),
-                rhs_scale=w_scales[0][:],
-                start=True,
-                stop=True,
-            )
-        xs_pick = kept("xs_pick", [P, S], U8, tag="x_table0")
-        nc.vector.tensor_copy(xs_pick[:], xs_table[:].indirect(offs_sb[:]))
         for a in range(TILES):
             h_pass(a, 0, 0)
-        for half in range(2):
-            gather_x(1, half)
+        for n in range(0, S, HALF):
+            nc.vector.tensor_copy(
+                x_last[:, n : n + HALF], x_table[1][:].indirect(offs_sb[:, n // GROUP : (n + HALF) // GROUP])
+            )
         es_pick = kept("es_pick", [P, V], U8, tag="x_table1")
         nc.vector.tensor_copy(es_pick[:], es_table[:].indirect(cen_sb[:]))
         e_pick = kept("e_pick", [P, V], U32, tag="es_table")
@@ -198,24 +202,23 @@ def tile_picked_ydec_tgt_p_kernel(
 
         state = [dict() for a in range(TILES)]
 
-        def wt(a, name, shape, dtype):
+        def staged(a, name, shape, dtype):
             state[a][name] = work.tile(shape, dtype, name=name, align_bytes=64)
             return state[a][name]
 
         def project(a):
-            h = h_banks[a]
-            for j in range(PACK):
+            for t in range(PACK):
                 for g in range(PASSES):
-                    if j or g:
-                        h_pass(a, j, g)
-            h_bf = wt(a, "h_bf", [P, P, PACK], BF16)
-            nc.scalar.copy(h_bf[:], h[:].rearrange("p j n -> p n j"))
+                    if t or g:
+                        h_pass(a, t, g)
+            h_bf = staged(a, "h_bf", [P, P, PACK], BF16)
+            nc.scalar.copy(h_bf[:], h_banks[a][:].rearrange("p t n -> p n t"))
 
         def inner(a):
             h_codes = kept("h_codes%d" % a, [P, P], U32, tag="h_codes_odd" if a % 2 else "e_table")
-            h_scales = wt(a, "h_scales", [P, P], U8)
+            h_scales = staged(a, "h_scales", [P, P], U8)
             nc.vector.quantize_mx(
-                out=h_codes[:].bitcast(FP8X4), scales=h_scales[:], in_=state[a]["h_bf"][:].rearrange("p n j -> p (n j)")
+                out=h_codes[:].bitcast(FP8X4), scales=h_scales[:], in_=state[a]["h_bf"][:].rearrange("p n t -> p (n t)")
             )
             y = psum.tile([P, 2 * V], F32, name="y", tag="y")
             state[a]["y"] = y
@@ -230,31 +233,29 @@ def tile_picked_ydec_tgt_p_kernel(
             )
 
         def distance(a):
-            part = wt(a, "part", [P, V], F32)
+            part = staged(a, "part", [P, V], F32)
             nc.vector.scalar_tensor_tensor(part[:], state[a]["y"][:, 0:V], -0.2, qn_wide, ALU.mult, ALU.add)
             root = pair.tile([P, V], F32, name="root", align_bytes=64)
-            nc.scalar.activation(
-                root[:], part[:], ACT.Abs_reciprocal_sqrt, bias=beta[:, a : a + 1], scale=alpha[:]
-            )
-            kern = wt(a, "kern", [P, V], F32)
+            nc.scalar.activation(root[:], part[:], ACT.Abs_reciprocal_sqrt, bias=beta[:, a : a + 1], scale=alpha[:])
+            kern = staged(a, "kern", [P, V], F32)
             nc.scalar.activation(kern[:], root[:], ACT.Square)
 
         def weigh(a):
             kern = state[a]["kern"]
-            rr = wt(a, "rr", [P, V], F32)
-            rr_sum = wt(a, "rr_sum", [P, 1], F32)
-            left = wt(a, "left", [P, V], F32)
+            rr = staged(a, "rr", [P, V], F32)
+            rr_sum = staged(a, "rr_sum", [P, 1], F32)
+            left = staged(a, "left", [P, V], F32)
             nc.vector.tensor_tensor(left[:], c_wide, kern[:], ALU.mult)
             nc.vector.scalar_tensor_tensor(rr[:], kern[:], 1.0, left[:], ALU.mult, ALU.mult, accum_out=rr_sum[:])
 
         def finish(a):
-            norm2 = wt(a, "norm2", [P, 1], F32)
-            nc.vector.reciprocal(norm2[:], state[a]["rr_sum"][:])
-            res = wt(a, "res", [P, V], F32)
+            norm = staged(a, "norm", [P, 1], F32)
+            nc.vector.reciprocal(norm[:], state[a]["rr_sum"][:])
+            res = staged(a, "res", [P, V], F32)
             if a < TILES - 1:
-                nc.scalar.activation(res[:], state[a]["rr"][:], ACT.Copy, scale=norm2[:])
+                nc.scalar.activation(res[:], state[a]["rr"][:], ACT.Copy, scale=norm[:])
             else:
-                nc.vector.tensor_scalar_mul(res[:], state[a]["rr"][:], norm2[:])
+                nc.vector.tensor_scalar_mul(res[:], state[a]["rr"][:], norm[:])
             nc.sync.dma_start(out[a * P : (a + 1) * P, :], res[:])
 
         stages = [project, inner, distance, weigh, finish]

@@ -15,7 +15,6 @@ U8 = mybir.dt.uint8
 FP8X4 = mybir.dt.float8_e4m3fn_x4
 ALU = mybir.AluOpType
 ACT = mybir.ActivationFunctionType
-AXIS = mybir.AxisListType
 
 P = 128
 PACK = 4
@@ -24,10 +23,20 @@ PASSES = K // K_PASS
 TILES = S // P
 HALF = S // 2
 GROUP = 16
-SCALE_ROWS = 4
+QUAD = 32
+QUADS = P // QUAD
+ROWS = 4
+PASS_ROWS = QUADS * ROWS
 V_BLOCKS = V // P
 LAST = P - 1
-ROUND_ON_SCALAR = (80, 48)
+XS_ROW = P - QUAD
+XS_FIRST = (12, 4)
+ES_STEP = P // PASS_ROWS
+ROUND_ON_SCALAR = 44
+SQUARE_ON_SCALAR = (2, 3)
+SCALE_ON_SCALAR = 2
+Y_BANKS = (4, 5, 6, 0)
+C_BANK = 7
 
 
 def tile_picked_ydec_tgt_p_kernel(
@@ -36,230 +45,270 @@ def tile_picked_ydec_tgt_p_kernel(
     nc = tc.nc
     with ExitStack() as ctx:
         keep = ctx.enter_context(tc.tile_pool(name="keep", bufs=1))
-        work = ctx.enter_context(tc.tile_pool(name="work", bufs=TILES))
-        pair = ctx.enter_context(tc.tile_pool(name="pair", bufs=2))
-        psum = ctx.enter_context(tc.psum_pool(name="psum", bufs=4))
-        banks = ctx.enter_context(tc.psum_pool(name="banks", bufs=TILES))
+        laid = ctx.enter_context(tc.tile_pool(name="laid", bufs=1))
+        psum = ctx.enter_context(tc.psum_pool(name="psum", bufs=1))
 
         def kept(name, shape, dtype, tag=None):
             return keep.tile(shape, dtype, name=name, tag=tag or name, align_bytes=64)
 
+        def placed(name, shape, dtype, offset):
+            return laid.tile(shape, dtype, name=name, align_bytes=64, offset=offset)
+
+        def bank(name, shape, number):
+            return psum.tile(shape, F32, name=name, tag="bank%d" % number)
+
+        def as_words(access):
+            return access.bitcast(I32)
+
         offs_sb = kept("offs_sb", [P, S // GROUP], U16)
         cen_sb = kept("cen_sb", [P, V // GROUP], U16)
-        mass_row = kept("mass_row", [1, V], F32)
-        inv_row = kept("inv_row", [1, V], F32)
+        rows = kept("rows", [P, V], F32)
         own_rows = kept("own_rows", [P, P], F32)
-        xs_table = kept("xs_table", [P, T], U8)
-        es_table = kept("es_table", [P, W], U8)
         qn_table = kept("qn_table", [P, W], F32)
-        c_rows = kept("c_rows", [P, V], F32)
         ident = kept("ident", [P, P], F32)
-        w_raw = [kept("w_raw%d" % g, [P, PACK, H], F32) for g in range(PASSES)]
-        x_table = [kept("x_table%d" % g, [P, T], U32) for g in range(PASSES)]
-        e_table = kept("e_table", [P, W], U32)
+        border = PACK * T
+        xs_table = placed("xs_table", [P, T], U8, border - T // 2)
+        es_table = kept("es_table", [P, W], U8)
+        xs_plane = [kept("xs_plane%d" % g, [P, S], U8) for g in range(PASSES)]
+        es_plane = kept("es_plane", [P, V], U8)
+        w_raw = [kept("w_raw0", [P, PACK, H], F32)]
+        x_table = [kept("x_table0", [P, T], U32)]
 
-        nc.vector.memset(xs_table[:].bitcast(I32), 0)
-        nc.vector.memset(es_table[:].bitcast(I32), 0)
+        nc.gpsimd.memset(as_words(xs_table[0:XS_ROW, :]), 0)
+        nc.vector.memset(as_words(es_table[:]), 0)
+        nc.vector.memset(as_words(es_plane[:]), 0)
+        nc.vector.memset(as_words(xs_plane[1][:]), 0)
         nc.vector.memset(own_rows[0 : P - TILES, :], 0.0)
-        nc.vector.memset(c_rows[:], 0.0)
-        nc.gpsimd.memset(qn_table[0:LAST, :], 0.0)
+        nc.vector.memset(rows[0 : P - 2, :], 0.0)
+        nc.vector.memset(qn_table[0:LAST, :], 0.0)
         make_identity(nc, ident[:])
 
         def load_w(g):
             nc.sync.dma_start(w_raw[g][:], w1[g * K_PASS : (g + 1) * K_PASS, :].rearrange("(p j) c -> p j c", j=PACK))
 
         def load_words(table, words):
-            nc.sync.dma_start(table[:].bitcast(I32), words.rearrange("p n t -> p (n t)").bitcast(I32))
+            nc.sync.dma_start(as_words(table[:]), as_words(words.rearrange("p n t -> p (n t)")))
 
-        def load_scales(table, scales, q, first, count):
-            row = 32 * q + SCALE_ROWS * first
-            nc.sync.dma_start(
-                table[row : row + SCALE_ROWS * count, :].bitcast(I32),
-                scales[first : first + count, SCALE_ROWS * q : SCALE_ROWS * (q + 1), :].bitcast(I32),
-            )
+        def move_rows(target, source):
+            nc.sync.dma_start(as_words(target), as_words(source))
 
-        nc.sync.dma_start(cen_sb[:], cen)
-        load_w(0)
-        nc.scalar.dma_start(qn_table[LAST:P, :], qn[0:1, :])
-        nc.scalar.dma_start(mass_row[:], mass[0:1, :])
-        nc.scalar.dma_start(inv_row[:], inv[0:1, :])
-        nc.sync.dma_start(own_rows[P - TILES : P, :], own.rearrange("(a m) o -> a (m o)", m=P))
         nc.sync.dma_start(offs_sb[:], offs)
+        nc.scalar.dma_start(as_words(xs_table[XS_ROW:P, :]), as_words(x_scales.rearrange("g r n -> (g r) n")))
+        nc.sync.dma_start(cen_sb[:], cen)
+        nc.scalar.dma_start(qn_table[LAST:P, :], qn[0:1, :])
+        load_w(0)
+        nc.scalar.dma_start(rows[P - 2 : LAST, :], mass[0:1, :])
+        nc.scalar.dma_start(rows[LAST:P, :], inv[0:1, :])
+        nc.scalar.dma_start(own_rows[P - TILES : P, :], own.rearrange("(a m) o -> a (m o)", m=P))
+        nc.sync.dma_start(as_words(es_table[0:P:ES_STEP, :]), as_words(e_scales[0]))
         load_words(x_table[0], x_words[0])
-        for q in (0, 2):
-            for g in range(PASSES):
-                load_scales(xs_table, x_scales, q, g, 1)
-        for q in (1, 3):
-            load_scales(xs_table, x_scales, q, 0, PASSES)
-        load_w(1)
-        load_words(x_table[1], x_words[1])
-        for q in (0, 2, 1, 3):
-            load_scales(es_table, e_scales, q, 0, 1)
-        load_words(e_table, e_words[0])
+        xs_pick = kept("xs_pick", [P, S], U8)
+        nc.vector.tensor_copy(xs_pick[:], xs_table[:].indirect(offs_sb[:]))
 
-        mass_sum = kept("mass_sum", [1, 1], F32)
-        nc.vector.tensor_reduce(mass_sum[:], mass_row[:], AXIS.X, ALU.add, apply_absolute_value=True)
-        mass_root = kept("mass_root", [1, 1], F32)
-        nc.scalar.activation(mass_root[:], mass_sum[:], ACT.Abs_reciprocal_sqrt)
+        nc.vector.tensor_copy(as_words(xs_plane[0][:]), as_words(xs_pick[:]))
+
+        def move_quadrant(q):
+            row = QUAD * q + XS_FIRST[0]
+            move_rows(xs_plane[0][row : row + ROWS, :], xs_pick[XS_ROW + ROWS * q : XS_ROW + ROWS * (q + 1), :])
+
+        move_quadrant(0)
+        w_raw.append(placed("w_raw1", [P, PACK, H], F32, 0))
+        load_w(1)
+        for q in range(1, QUADS - 1):
+            move_quadrant(q)
+        x_table.append(placed("x_table1", [P, T], U32, border))
+        load_words(x_table[1], x_words[1])
+        for j in range(ROWS):
+            move_rows(xs_plane[1][XS_FIRST[1] + j : P : QUAD, :], xs_pick[XS_ROW + PASS_ROWS + j : P : ROWS, :])
+
         qn_pick = kept("qn_pick", [P, V], F32)
         nc.vector.tensor_copy(qn_pick[:], qn_table[:].indirect(cen_sb[:]))
-        share = kept("share", [1, V], F32)
-        nc.vector.tensor_scalar(share[:], mass_row[:], mass_root[:], mass_root[:], ALU.mult, ALU.mult)
-        share_inv = kept("share_inv", [1, V], F32)
-        nc.vector.tensor_tensor(share_inv[:], share[:], inv_row[:], ALU.mult)
-        nc.vector.tensor_tensor(c_rows[0:1, :], share_inv[:], share[:], ALU.mult)
 
-        w_bf = []
-        w_codes = []
-        w_scales = []
+        def turn(target, source):
+            for b in range(V_BLOCKS):
+                nc.tensor.transpose(target[:, b, :], source[:, b * P : (b + 1) * P], ident[:])
 
-        def round_w(g, tag):
-            w_bf.append(kept("w_bf%d" % g, [P, PACK * H], BF16, tag=tag))
-            dst = w_bf[g][:].rearrange("p (t m j) -> p m t j", t=PACK, j=PACK)
-            src = w_raw[g][:].rearrange("p j (m t) -> p m t j", t=PACK)
-            split = ROUND_ON_SCALAR[g]
-            nc.scalar.copy(dst[:, 0:split], src[:, 0:split])
-            nc.vector.tensor_copy(dst[:, split:P], src[:, split:P])
+        def spread(target, columns):
+            for b in range(V_BLOCKS):
+                nc.tensor.transpose(target[:, b * P : (b + 1) * P], columns[b].to_broadcast([P, P]), ident[:])
 
-        def quantize_w(g):
-            w_codes.append(kept("w_codes%d" % g, [P, H], U32))
-            w_scales.append(kept("w_scales%d" % g, [P, H], U8))
-            nc.vector.quantize_mx(out=w_codes[g][:].bitcast(FP8X4), scales=w_scales[g][:], in_=w_bf[g][:])
+        ones = kept("ones", [P, 1], F32)
+        nc.vector.memset(ones[:], 1.0)
+        one = kept("one", [P, 1], F32)
+        nc.scalar.activation(one[:], ones[:], ACT.Abs_reciprocal_sqrt)
 
-        round_w(0, None)
-        quantize_w(0)
-        x_first = kept("x_first", [P, S], U32, tag="w_bf0")
-        nc.vector.tensor_copy(x_first[:], x_table[0][:].indirect(offs_sb[:]))
-
-        turn = psum.tile([P, V_BLOCKS + 1, P], F32, name="turn", tag="y")
-        nc.tensor.transpose(turn[:, V_BLOCKS, :], own_rows[:], ident[:])
-        for b in range(V_BLOCKS):
-            nc.tensor.transpose(turn[:, b, :], qn_pick[:, b * P : (b + 1) * P], ident[:])
-        own_cols = turn[:, V_BLOCKS, P - TILES : P]
-        cols = kept("cols", [P, 2 * V_BLOCKS + 2 * TILES + 1], F32, tag="w_raw0")
-        qn_cols = cols[:, 0:V_BLOCKS]
-        c_cols = cols[:, V_BLOCKS : 2 * V_BLOCKS]
-        own1 = cols[:, 2 * V_BLOCKS : 2 * V_BLOCKS + TILES]
-        own_abs = cols[:, 2 * V_BLOCKS + TILES : 2 * V_BLOCKS + 2 * TILES]
-        own_sum = cols[:, 2 * V_BLOCKS + 2 * TILES :]
-        nc.scalar.copy(qn_cols, turn[:, 0:V_BLOCKS, LAST])
-        nc.scalar.activation(own1, own_cols, ACT.Copy, bias=1.0)
-        nc.scalar.activation(own_abs, own_cols, ACT.Abs, accum_out=own_sum)
-        c_turn = psum.tile([P, V_BLOCKS, P], F32, name="c_turn", tag="y")
-        for b in range(V_BLOCKS):
-            nc.tensor.transpose(c_turn[:, b, :], c_rows[:, b * P : (b + 1) * P], ident[:])
-        nc.scalar.copy(c_cols, c_turn[:, :, 0])
-        spread = [banks.tile([P, P], F32, name="spread", tag="h") for b in range(2 * V_BLOCKS)]
-        for b in range(2 * V_BLOCKS):
-            nc.tensor.transpose(spread[b][:], cols[:, b : b + 1].to_broadcast([P, P]), ident[:])
-
-        xs_pick = kept("xs_pick", [P, S], U8, tag="x_table0")
-        nc.vector.tensor_copy(xs_pick[:], xs_table[:].indirect(offs_sb[:]))
-        round_w(1, "xs_table")
-        quantize_w(1)
-        x_last = kept("x_last", [P, S], U32, tag="xs_table")
-        x_pick = (x_first, x_last)
-
-        wide = kept("wide", [P, 2 * V], F32, tag="w_raw1")
-        for b in range(2 * V_BLOCKS):
-            nc.scalar.copy(wide[:, b * P : (b + 1) * P], spread[b][:])
-        qn_wide = wide[:, 0:V]
-        c_wide = wide[:, V : 2 * V]
-
+        qn_turn = bank("qn_turn", [P, V_BLOCKS, P], 4)
+        turn(qn_turn, qn_pick)
+        qn_cols = kept("qn_cols", [P, V_BLOCKS], F32)
+        nc.scalar.copy(qn_cols[:], qn_turn[:, :, LAST])
+        qn_spread = bank("qn_spread", [P, V], 5)
+        spread(qn_spread, [qn_cols[:, b : b + 1] for b in range(V_BLOCKS)])
+        qn_wide = kept("qn_wide", [P, V], F32)
+        nc.scalar.copy(qn_wide[:], qn_spread[:])
         qn_abs = kept("qn_abs", [P, V], F32)
         qn_mean = kept("qn_mean", [P, 1], F32)
-        nc.scalar.activation(qn_abs[:], qn_wide, ACT.Abs, scale=1.0 / V, accum_out=qn_mean[:])
+        nc.scalar.activation(qn_abs[:], qn_wide[:], ACT.Abs, scale=1.0 / V, accum_out=qn_mean[:])
+
+        rows_turn = bank("rows_turn", [P, V_BLOCKS, P], 6)
+        turn(rows_turn, rows)
+        cols = kept("cols", [P, V_BLOCKS, 2], F32)
+        nc.scalar.copy(cols[:], rows_turn[:, :, P - 2 : P])
+        mass_spread = bank("mass_spread", [P, V], 2)
+        spread(mass_spread, [cols[:, b, 0:1] for b in range(V_BLOCKS)])
+        mass_abs = kept("mass_abs", [P, V], F32)
+        mass_sum = kept("mass_sum", [P, 1], F32)
+        nc.scalar.activation(mass_abs[:], mass_spread[:], ACT.Abs, accum_out=mass_sum[:])
+        mass_root = kept("mass_root", [P, 1], F32)
+        nc.scalar.activation(mass_root[:], mass_sum[:], ACT.Abs_reciprocal_sqrt)
+        mass_sq = kept("mass_sq", [P, V_BLOCKS], F32)
+        nc.scalar.activation(mass_sq[:], cols[:, :, 0], ACT.Square, scale=mass_root[:])
+        c_cols = kept("c_cols", [P, V_BLOCKS], F32)
+        for b in range(V_BLOCKS):
+            nc.scalar.activation(c_cols[:, b : b + 1], mass_sq[:, b : b + 1], ACT.Copy, scale=cols[:, b, 1:2])
+        c_wide = bank("c_wide", [P, V], C_BANK)
+        spread(c_wide, [c_cols[:, b : b + 1] for b in range(V_BLOCKS)])
+
+        own_turn = bank("own_turn", [P, P], 6)
+        nc.tensor.transpose(own_turn[:], own_rows[:], ident[:])
+        own_cols = own_turn[:, P - TILES : P]
+        own_work = kept("own_work", [P, 2, TILES], F32)
+        own1 = own_work[:, 0, :]
+        nc.scalar.activation(own1, own_cols, ACT.Identity, bias=one[:])
+        own_sum = kept("own_sum", [P, 1], F32)
+        nc.scalar.activation(own_work[:, 1, :], own_cols, ACT.Abs, accum_out=own_sum[:])
         size = kept("size", [P, 1], F32)
-        nc.scalar.activation(size[:], own_sum, ACT.Identity, bias=qn_mean[:])
+        nc.scalar.activation(size[:], own_sum[:], ACT.Identity, bias=qn_mean[:])
         alpha = kept("alpha", [P, 1], F32)
         nc.scalar.activation(alpha[:], size[:], ACT.Abs_reciprocal_sqrt, bias=1.0)
         beta = kept("beta", [P, TILES], F32)
         nc.scalar.activation(beta[:], own1, ACT.Copy, scale=alpha[:])
 
-        h_banks = [banks.tile([P, PACK, P], F32, name="h", tag="h") for a in range(TILES)]
+        w_codes = []
+        w_scales = []
 
-        def h_pass(a, t, g):
-            nc.tensor.matmul_mx(
-                out=h_banks[a][:, t, :],
-                lhsT=w_codes[g][:, t * P : (t + 1) * P].bitcast(FP8X4),
-                lhsT_scale=w_scales[g][:, t * P : (t + 1) * P],
-                rhs=x_pick[g][:, a * P : (a + 1) * P].bitcast(FP8X4),
-                rhs_scale=xs_pick[SCALE_ROWS * g : P, a * P : (a + 1) * P],
-                start=(g == 0),
-                stop=(g == PASSES - 1),
-            )
+        def quantize_w(g, tag):
+            w_bf = kept("w_bf%d" % g, [P, PACK * H], BF16, tag=tag)
+            dst = w_bf[:].rearrange("p (t m j) -> p m t j", t=PACK, j=PACK)
+            src = w_raw[g][:].rearrange("p j (m t) -> p m t j", t=PACK)
+            nc.scalar.copy(dst[:, 0:ROUND_ON_SCALAR], src[:, 0:ROUND_ON_SCALAR])
+            nc.vector.tensor_copy(dst[:, ROUND_ON_SCALAR:P], src[:, ROUND_ON_SCALAR:P])
+            w_codes.append(kept("w_codes%d" % g, [P, H], U32))
+            w_scales.append(kept("w_scales%d" % g, [P, H], U8))
+            nc.vector.quantize_mx(out=w_codes[g][:].bitcast(FP8X4), scales=w_scales[g][:], in_=w_bf[:])
 
-        for a in range(TILES):
-            h_pass(a, 0, 0)
-        for n in range(0, S, HALF):
+        quantize_w(0, None)
+        e_table = kept("e_table", [P, W], U32, tag="w_bf0")
+        load_words(e_table, e_words[0])
+
+        h_banks = [bank("h", [P, PACK, P], a) for a in range(TILES)]
+        x_pick = [kept("x_pick%d" % g, [P, S], U32) for g in range(PASSES)]
+
+        def gather_x(g, n):
             nc.vector.tensor_copy(
-                x_last[:, n : n + HALF], x_table[1][:].indirect(offs_sb[:, n // GROUP : (n + HALF) // GROUP])
+                x_pick[g][:, n : n + HALF], x_table[g][:].indirect(offs_sb[:, n // GROUP : (n + HALF) // GROUP])
             )
-        es_pick = kept("es_pick", [P, V], U8, tag="x_table1")
+
+        def project(a, g):
+            for t in range(PACK):
+                nc.tensor.matmul_mx(
+                    out=h_banks[a][:, t, :],
+                    lhsT=w_codes[g][:, t * P : (t + 1) * P].bitcast(FP8X4),
+                    lhsT_scale=w_scales[g][:, t * P : (t + 1) * P],
+                    rhs=x_pick[g][:, a * P : (a + 1) * P].bitcast(FP8X4),
+                    rhs_scale=xs_plane[g][XS_FIRST[g] : P, a * P : (a + 1) * P],
+                    start=(g == 0 and t == 0),
+                    stop=(g == PASSES - 1 and t == PACK - 1),
+                )
+
+        for n in range(0, S, HALF):
+            gather_x(0, n)
+        es_pick = kept("es_pick", [P, V], U8, tag="x_table0")
         nc.vector.tensor_copy(es_pick[:], es_table[:].indirect(cen_sb[:]))
-        e_pick = kept("e_pick", [P, V], U32, tag="es_table")
+        for j in range(ROWS):
+            move_rows(es_plane[j:P:QUAD, :], es_pick[ES_STEP * j : P : QUAD, :])
+        for a in range(TILES):
+            project(a, 0)
+        quantize_w(1, "mass_sq")
+        for n in range(0, S, HALF):
+            gather_x(1, n)
+            for a in range(n // P, (n + HALF) // P):
+                project(a, 1)
+        e_pick = kept("e_pick", [P, V], U32)
         nc.vector.tensor_copy(e_pick[:], e_table[:].indirect(cen_sb[:]))
 
+        h_codes = kept("h_codes", [P, 2 * P], U32, tag="w_bf0")
+        h_scales = kept("h_scales", [P, S], U8)
         state = [dict() for a in range(TILES)]
 
         def staged(a, name, shape, dtype):
-            state[a][name] = work.tile(shape, dtype, name=name, align_bytes=64)
+            state[a][name] = kept("%s%d" % (name, a), shape, dtype)
             return state[a][name]
 
-        def project(a):
-            for t in range(PACK):
-                for g in range(PASSES):
-                    if t or g:
-                        h_pass(a, t, g)
+        def round_h(a):
             h_bf = staged(a, "h_bf", [P, P, PACK], BF16)
             nc.scalar.copy(h_bf[:], h_banks[a][:].rearrange("p t n -> p n t"))
 
         def inner(a):
-            h_codes = kept("h_codes%d" % a, [P, P], U32, tag="h_codes_odd" if a % 2 else "e_table")
-            h_scales = staged(a, "h_scales", [P, P], U8)
-            nc.vector.quantize_mx(
-                out=h_codes[:].bitcast(FP8X4), scales=h_scales[:], in_=state[a]["h_bf"][:].rearrange("p n t -> p (n t)")
-            )
-            y = psum.tile([P, 2 * V], F32, name="y", tag="y")
-            state[a]["y"] = y
+            codes = h_codes[:, a % 2 * P : (a % 2 + 1) * P].bitcast(FP8X4)
+            scales = h_scales[:, a * P : (a + 1) * P]
+            nc.vector.quantize_mx(out=codes, scales=scales, in_=state[a]["h_bf"][:].rearrange("p n t -> p (n t)"))
+            state[a]["y"] = bank("y", [P, V], Y_BANKS[a])
             nc.tensor.matmul_mx(
-                out=y[:, 0:V],
-                lhsT=h_codes[:].bitcast(FP8X4),
-                lhsT_scale=h_scales[:],
+                out=state[a]["y"][:],
+                lhsT=codes,
+                lhsT_scale=scales,
                 rhs=e_pick[:].bitcast(FP8X4),
-                rhs_scale=es_pick[:],
+                rhs_scale=es_plane[:],
                 start=True,
                 stop=True,
             )
 
         def distance(a):
             part = staged(a, "part", [P, V], F32)
-            nc.vector.scalar_tensor_tensor(part[:], state[a]["y"][:, 0:V], -0.2, qn_wide, ALU.mult, ALU.add)
-            root = pair.tile([P, V], F32, name="root", align_bytes=64)
-            nc.scalar.activation(root[:], part[:], ACT.Abs_reciprocal_sqrt, bias=beta[:, a : a + 1], scale=alpha[:])
+            nc.vector.scalar_tensor_tensor(part[:], state[a]["y"][:], -0.2, qn_wide[:], ALU.mult, ALU.add)
+
+        def inverse_root(a):
+            root = staged(a, "root", [P, V], F32)
+            nc.scalar.activation(
+                root[:], state[a]["part"][:], ACT.Abs_reciprocal_sqrt, bias=beta[:, a : a + 1], scale=alpha[:]
+            )
+
+        def kernel_value(a):
             kern = staged(a, "kern", [P, V], F32)
-            nc.scalar.activation(kern[:], root[:], ACT.Square)
+            nc.scalar.activation(kern[:], state[a]["root"][:], ACT.Square)
+
+        def first_factor(a):
+            kern = state[a]["kern"]
+            left = staged(a, "left", [P, V], F32)
+            if a in SQUARE_ON_SCALAR:
+                nc.scalar.activation(left[:], kern[:], ACT.Square)
+                state[a]["right"] = c_wide
+            else:
+                nc.vector.tensor_tensor(left[:], kern[:], c_wide[:], ALU.mult)
+                state[a]["right"] = kern
 
         def weigh(a):
-            kern = state[a]["kern"]
             rr = staged(a, "rr", [P, V], F32)
             rr_sum = staged(a, "rr_sum", [P, 1], F32)
-            left = staged(a, "left", [P, V], F32)
-            nc.vector.tensor_tensor(left[:], c_wide, kern[:], ALU.mult)
-            nc.vector.scalar_tensor_tensor(rr[:], kern[:], 1.0, left[:], ALU.mult, ALU.mult, accum_out=rr_sum[:])
+            nc.vector.scalar_tensor_tensor(
+                rr[:], state[a]["left"][:], 1.0, state[a]["right"][:], ALU.mult, ALU.mult, accum_out=rr_sum[:]
+            )
 
-        def finish(a):
+        def invert(a):
             norm = staged(a, "norm", [P, 1], F32)
             nc.vector.reciprocal(norm[:], state[a]["rr_sum"][:])
+
+        def finish(a):
             res = staged(a, "res", [P, V], F32)
-            if a < TILES - 1:
-                nc.scalar.activation(res[:], state[a]["rr"][:], ACT.Copy, scale=norm[:])
+            if a == SCALE_ON_SCALAR:
+                nc.scalar.activation(res[:], state[a]["rr"][:], ACT.Copy, scale=state[a]["norm"][:])
             else:
-                nc.vector.tensor_scalar_mul(res[:], state[a]["rr"][:], norm[:])
+                nc.vector.tensor_scalar_mul(res[:], state[a]["rr"][:], state[a]["norm"][:])
             nc.sync.dma_start(out[a * P : (a + 1) * P, :], res[:])
 
-        stages = [project, inner, distance, weigh, finish]
-        for step in range(TILES + len(stages) - 1):
-            for s in reversed(range(len(stages))):
-                if 0 <= step - s < TILES:
-                    stages[s](step - s)
+        stages = [(0, round_h), (1, inner), (2, distance)]
+        stages.extend(enumerate([inverse_root, kernel_value, first_factor, weigh, invert, finish], TILES))
+        for step in range(stages[-1][0] + TILES):
+            for lag, stage in stages:
+                if 0 <= step - lag < TILES:
+                    stage(step - lag)

@@ -34,7 +34,7 @@ XS_FIRST = (12, 4)
 ES_STEP = P // PASS_ROWS
 ROUND_ON_SCALAR = 44
 SQUARE_ON_SCALAR = (2, 3)
-SCALE_ON_SCALAR = 2
+SCALE_ON_SCALAR = (0, 1)
 Y_BANKS = (4, 5, 6, 0)
 C_BANK = 7
 
@@ -203,9 +203,9 @@ def tile_picked_ydec_tgt_p_kernel(
         h_banks = [bank("h", [P, PACK, P], a) for a in range(TILES)]
         x_pick = [kept("x_pick%d" % g, [P, S], U32) for g in range(PASSES)]
 
-        def gather_x(g, n):
+        def gather_x(g, n, count=HALF):
             nc.vector.tensor_copy(
-                x_pick[g][:, n : n + HALF], x_table[g][:].indirect(offs_sb[:, n // GROUP : (n + HALF) // GROUP])
+                x_pick[g][:, n : n + count], x_table[g][:].indirect(offs_sb[:, n // GROUP : (n + count) // GROUP])
             )
 
         def project(a, g):
@@ -229,10 +229,9 @@ def tile_picked_ydec_tgt_p_kernel(
         for a in range(TILES):
             project(a, 0)
         quantize_w(1, "mass_sq")
-        for n in range(0, S, HALF):
-            gather_x(1, n)
-            for a in range(n // P, (n + HALF) // P):
-                project(a, 1)
+        for a in range(TILES):
+            gather_x(1, a * P, P)
+            project(a, 1)
         e_pick = kept("e_pick", [P, V], U32)
         nc.vector.tensor_copy(e_pick[:], e_table[:].indirect(cen_sb[:]))
 
@@ -240,8 +239,8 @@ def tile_picked_ydec_tgt_p_kernel(
         h_scales = kept("h_scales", [P, S], U8)
         state = [dict() for a in range(TILES)]
 
-        def staged(a, name, shape, dtype):
-            state[a][name] = kept("%s%d" % (name, a), shape, dtype)
+        def staged(a, name, shape, dtype, tag=None):
+            state[a][name] = kept("%s%d" % (name, a), shape, dtype, tag)
             return state[a][name]
 
         def round_h(a):
@@ -279,7 +278,7 @@ def tile_picked_ydec_tgt_p_kernel(
 
         def first_factor(a):
             kern = state[a]["kern"]
-            left = staged(a, "left", [P, V], F32)
+            left = staged(a, "left", [P, V], F32, "part3" if a == 2 else None)
             if a in SQUARE_ON_SCALAR:
                 nc.scalar.activation(left[:], kern[:], ACT.Square)
                 state[a]["right"] = c_wide
@@ -288,19 +287,19 @@ def tile_picked_ydec_tgt_p_kernel(
                 state[a]["right"] = kern
 
         def weigh(a):
-            rr = staged(a, "rr", [P, V], F32)
+            rr = staged(a, "rr", [P, V], F32, "root1" if a == 0 else None)
             rr_sum = staged(a, "rr_sum", [P, 1], F32)
             nc.vector.scalar_tensor_tensor(
                 rr[:], state[a]["left"][:], 1.0, state[a]["right"][:], ALU.mult, ALU.mult, accum_out=rr_sum[:]
             )
 
         def invert(a):
-            norm = staged(a, "norm", [P, 1], F32)
+            norm = staged(a, "norm", [P, 1], F32, "kern%d" % (a + 1) if a in (1, 2) else None)
             nc.vector.reciprocal(norm[:], state[a]["rr_sum"][:])
 
         def finish(a):
             res = staged(a, "res", [P, V], F32)
-            if a == SCALE_ON_SCALAR:
+            if a in SCALE_ON_SCALAR:
                 nc.scalar.activation(res[:], state[a]["rr"][:], ACT.Copy, scale=state[a]["norm"][:])
             else:
                 nc.vector.tensor_scalar_mul(res[:], state[a]["rr"][:], state[a]["norm"][:])

@@ -197,7 +197,7 @@ def tile_picked_ydec_tgt_p_kernel(
             nc.vector.quantize_mx(out=w_codes[g][:].bitcast(FP8X4), scales=w_scales[g][:], in_=w_bf[:])
 
         quantize_w(0, None)
-        e_table = kept("e_table", [P, W], U32, tag="w_bf0")
+        e_table = kept("e_table", [P, W], U32, tag="qn_table")
         load_words(e_table, e_words[0])
 
         h_banks = [bank("h", [P, PACK, P], a) for a in range(TILES)]
@@ -222,7 +222,7 @@ def tile_picked_ydec_tgt_p_kernel(
 
         for n in range(0, S, HALF):
             gather_x(0, n)
-        es_pick = kept("es_pick", [P, V], U8, tag="x_table0")
+        es_pick = kept("es_pick", [P, V], U8, tag="w_bf0")
         nc.vector.tensor_copy(es_pick[:], es_table[:].indirect(cen_sb[:]))
         for j in range(ROWS):
             move_rows(es_plane[j:P:QUAD, :], es_pick[ES_STEP * j : P : QUAD, :])
@@ -235,7 +235,7 @@ def tile_picked_ydec_tgt_p_kernel(
         e_pick = kept("e_pick", [P, V], U32)
         nc.vector.tensor_copy(e_pick[:], e_table[:].indirect(cen_sb[:]))
 
-        h_codes = kept("h_codes", [P, 2 * P], U32, tag="w_bf0")
+        h_codes = kept("h_codes", [P, 2 * P], U32, tag="qn_table")
         h_scales = kept("h_scales", [P, S], U8)
         state = [dict() for a in range(TILES)]
 

@@ -111,11 +111,10 @@ def tile_picked_ydec_tgt_p_kernel(
             row = QUAD * q + XS_FIRST[0]
             move_rows(xs_plane[0][row : row + ROWS, :], xs_pick[XS_ROW + ROWS * q : XS_ROW + ROWS * (q + 1), :])
 
-        move_quadrant(0)
+        for q in range(QUADS - 1):
+            move_quadrant(q)
         w_raw.append(placed("w_raw1", [P, PACK, H], F32, 0))
         load_w(1)
-        for q in range(1, QUADS - 1):
-            move_quadrant(q)
         x_table.append(placed("x_table1", [P, T], U32, border))
         load_words(x_table[1], x_words[1])
         for j in range(ROWS):
@@ -220,8 +219,7 @@ def tile_picked_ydec_tgt_p_kernel(
                     stop=(g == PASSES - 1 and t == PACK - 1),
                 )
 
-        for n in range(0, S, HALF):
-            gather_x(0, n)
+        gather_x(0, 0, S)
         es_pick = kept("es_pick", [P, V], U8, tag="w_bf0")
         nc.vector.tensor_copy(es_pick[:], es_table[:].indirect(cen_sb[:]))
         for j in range(ROWS):

@@ -33,9 +33,9 @@ XS_ROW = P - QUAD
 XS_FIRST = (12, 4)
 ES_STEP = P // PASS_ROWS
 ROUND_ON_SCALAR = 44
-SQUARE_ON_SCALAR = (2, 3)
+SQUARE_ON_VECTOR = (0, 1, 2)
 SCALE_ON_SCALAR = (0, 1)
-Y_BANKS = (4, 5, 6, 0)
+Y_BANKS = (4, 5, 6, 0, 1, 2, 3, 4)
 C_BANK = 7
 
 
@@ -233,7 +233,7 @@ def tile_picked_ydec_tgt_p_kernel(
         e_pick = kept("e_pick", [P, V], U32)
         nc.vector.tensor_copy(e_pick[:], e_table[:].indirect(cen_sb[:]))
 
-        h_codes = kept("h_codes", [P, 2 * P], U32, tag="qn_table")
+        h_codes = kept("h_codes", [P, S], U32, tag="qn_table")
         h_scales = kept("h_scales", [P, S], U8)
         state = [dict() for a in range(TILES)]
 
@@ -241,58 +241,72 @@ def tile_picked_ydec_tgt_p_kernel(
             state[a][name] = kept("%s%d" % (name, a), shape, dtype, tag)
             return state[a][name]
 
+        def block(b):
+            return slice(b * P, (b + 1) * P)
+
         def round_h(a):
             h_bf = staged(a, "h_bf", [P, P, PACK], BF16)
             nc.scalar.copy(h_bf[:], h_banks[a][:].rearrange("p t n -> p n t"))
 
         def inner(a):
-            codes = h_codes[:, a % 2 * P : (a % 2 + 1) * P].bitcast(FP8X4)
-            scales = h_scales[:, a * P : (a + 1) * P]
+            codes = h_codes[:, block(a)].bitcast(FP8X4)
+            scales = h_scales[:, block(a)]
             nc.vector.quantize_mx(out=codes, scales=scales, in_=state[a]["h_bf"][:].rearrange("p n t -> p (n t)"))
-            state[a]["y"] = bank("y", [P, V], Y_BANKS[a])
-            nc.tensor.matmul_mx(
-                out=state[a]["y"][:],
-                lhsT=codes,
-                lhsT_scale=scales,
-                rhs=e_pick[:].bitcast(FP8X4),
-                rhs_scale=es_plane[:],
-                start=True,
-                stop=True,
-            )
+            state[a]["y"] = []
+            for b in range(V_BLOCKS):
+                y = bank("y", [P, P], Y_BANKS[V_BLOCKS * a + b])
+                state[a]["y"].append(y)
+                nc.tensor.matmul_mx(
+                    out=y[:],
+                    lhsT=codes,
+                    lhsT_scale=scales,
+                    rhs=e_pick[:, block(b)].bitcast(FP8X4),
+                    rhs_scale=es_plane[:, block(b)],
+                    start=True,
+                    stop=True,
+                )
 
         def distance(a):
             part = staged(a, "part", [P, V], F32)
-            nc.vector.scalar_tensor_tensor(part[:], state[a]["y"][:], -0.2, qn_wide[:], ALU.mult, ALU.add)
+            for b in range(V_BLOCKS):
+                nc.vector.scalar_tensor_tensor(
+                    part[:, block(b)], state[a]["y"][b][:], -0.2, qn_wide[:, block(b)], ALU.mult, ALU.add
+                )
 
         def inverse_root(a):
             root = staged(a, "root", [P, V], F32)
-            nc.scalar.activation(
-                root[:], state[a]["part"][:], ACT.Abs_reciprocal_sqrt, bias=beta[:, a : a + 1], scale=alpha[:]
-            )
+            for b in range(V_BLOCKS):
+                nc.scalar.activation(
+                    root[:, block(b)],
+                    state[a]["part"][:, block(b)],
+                    ACT.Abs_reciprocal_sqrt,
+                    bias=beta[:, a : a + 1],
+                    scale=alpha[:],
+                )
 
         def kernel_value(a):
             kern = staged(a, "kern", [P, V], F32)
-            nc.scalar.activation(kern[:], state[a]["root"][:], ACT.Square)
+            for b in range(V_BLOCKS):
+                root = state[a]["root"][:, block(b)]
+                if a in SQUARE_ON_VECTOR:
+                    nc.vector.tensor_tensor(kern[:, block(b)], root, root, ALU.mult)
+                else:
+                    nc.scalar.activation(kern[:, block(b)], root, ACT.Square)
 
         def first_factor(a):
-            kern = state[a]["kern"]
-            left = staged(a, "left", [P, V], F32, "part3" if a == 2 else None)
-            if a in SQUARE_ON_SCALAR:
-                nc.scalar.activation(left[:], kern[:], ACT.Square)
-                state[a]["right"] = c_wide
-            else:
-                nc.vector.tensor_tensor(left[:], kern[:], c_wide[:], ALU.mult)
-                state[a]["right"] = kern
+            left = staged(a, "left", [P, V], F32)
+            for b in range(V_BLOCKS):
+                nc.scalar.activation(left[:, block(b)], state[a]["kern"][:, block(b)], ACT.Square)
 
         def weigh(a):
-            rr = staged(a, "rr", [P, V], F32, "root1" if a == 0 else None)
+            rr = staged(a, "rr", [P, V], F32)
             rr_sum = staged(a, "rr_sum", [P, 1], F32)
             nc.vector.scalar_tensor_tensor(
-                rr[:], state[a]["left"][:], 1.0, state[a]["right"][:], ALU.mult, ALU.mult, accum_out=rr_sum[:]
+                rr[:], state[a]["left"][:], 1.0, c_wide[:], ALU.mult, ALU.mult, accum_out=rr_sum[:]
             )
 
         def invert(a):
-            norm = staged(a, "norm", [P, 1], F32, "kern%d" % (a + 1) if a in (1, 2) else None)
+            norm = staged(a, "norm", [P, 1], F32)
             nc.vector.reciprocal(norm[:], state[a]["rr_sum"][:])
 
         def finish(a):
@@ -303,9 +317,13 @@ def tile_picked_ydec_tgt_p_kernel(
                 nc.vector.tensor_scalar_mul(res[:], state[a]["rr"][:], state[a]["norm"][:])
             nc.sync.dma_start(out[a * P : (a + 1) * P, :], res[:])
 
-        stages = [(0, round_h), (1, inner), (2, distance)]
-        stages.extend(enumerate([inverse_root, kernel_value, first_factor, weigh, invert, finish], TILES))
-        for step in range(stages[-1][0] + TILES):
-            for lag, stage in stages:
-                if 0 <= step - lag < TILES:
-                    stage(step - lag)
+        for stage in (round_h, inner, distance, inverse_root, kernel_value, first_factor):
+            for a in range(TILES):
+                stage(a)
+        for step in range(TILES + 1):
+            if step < TILES:
+                weigh(step)
+            if step > 0:
+                invert(step - 1)
+        for a in range(TILES):
+            finish(a)

@@ -33,10 +33,14 @@ XS_ROW = P - QUAD
 XS_FIRST = (12, 4)
 ES_STEP = P // PASS_ROWS
 ROUND_ON_SCALAR = 44
-SQUARE_ON_VECTOR = (0, 1, 2)
-SCALE_ON_SCALAR = (0, 1)
-Y_BANKS = (4, 5, 6, 0, 1, 2, 3, 4)
+FIRST = "VVVV"
+SECOND = "SSSS"
+SCALE = "SSVV"
+Y_BANKS = (4, 5, 6, 0)
 C_BANK = 7
+LATE = 2 * PACK * T
+ROUND_H_ON_VECTOR = 2
+TAKES = {"norm0":"kern1","norm1":"kern2","norm2":"kern3"}
 
 
 def tile_picked_ydec_tgt_p_kernel(
@@ -64,7 +68,7 @@ def tile_picked_ydec_tgt_p_kernel(
         cen_sb = kept("cen_sb", [P, V // GROUP], U16)
         rows = kept("rows", [P, V], F32)
         own_rows = kept("own_rows", [P, P], F32)
-        qn_table = kept("qn_table", [P, W], F32)
+        qn_table = placed("qn_table", [P, W], F32, LATE)
         ident = kept("ident", [P, P], F32)
         border = PACK * T
         xs_table = placed("xs_table", [P, T], U8, border - T // 2)
@@ -187,8 +191,8 @@ def tile_picked_ydec_tgt_p_kernel(
 
         def quantize_w(g, tag):
             w_bf = kept("w_bf%d" % g, [P, PACK * H], BF16, tag=tag)
-            dst = w_bf[:].rearrange("p (t m j) -> p m t j", t=PACK, j=PACK)
-            src = w_raw[g][:].rearrange("p j (m t) -> p m t j", t=PACK)
+            dst = w_bf[:].rearrange("p (t m j) -> p m j t", t=PACK, j=PACK)
+            src = w_raw[g][:].rearrange("p j (m t) -> p m j t", t=PACK)
             nc.scalar.copy(dst[:, 0:ROUND_ON_SCALAR], src[:, 0:ROUND_ON_SCALAR])
             nc.vector.tensor_copy(dst[:, ROUND_ON_SCALAR:P], src[:, ROUND_ON_SCALAR:P])
             w_codes.append(kept("w_codes%d" % g, [P, H], U32))
@@ -196,7 +200,7 @@ def tile_picked_ydec_tgt_p_kernel(
             nc.vector.quantize_mx(out=w_codes[g][:].bitcast(FP8X4), scales=w_scales[g][:], in_=w_bf[:])
 
         quantize_w(0, None)
-        e_table = kept("e_table", [P, W], U32, tag="qn_table")
+        e_table = placed("e_table", [P, W], U32, LATE)
         load_words(e_table, e_words[0])
 
         h_banks = [bank("h", [P, PACK, P], a) for a in range(TILES)]
@@ -227,82 +231,80 @@ def tile_picked_ydec_tgt_p_kernel(
         for a in range(TILES):
             project(a, 0)
         quantize_w(1, "mass_sq")
-        for a in range(TILES):
-            gather_x(1, a * P, P)
-            project(a, 1)
+        for tiles in [[0],[1],[2,3]]:
+            gather_x(1, tiles[0] * P, len(tiles) * P)
+            for a in tiles:
+                project(a, 1)
         e_pick = kept("e_pick", [P, V], U32)
         nc.vector.tensor_copy(e_pick[:], e_table[:].indirect(cen_sb[:]))
-
-        h_codes = kept("h_codes", [P, S], U32, tag="qn_table")
+        h_codes = placed("h_codes", [P, S], U32, LATE)
         h_scales = kept("h_scales", [P, S], U8)
         state = [dict() for a in range(TILES)]
 
-        def staged(a, name, shape, dtype, tag=None):
-            state[a][name] = kept("%s%d" % (name, a), shape, dtype, tag)
+        def staged(a, name, shape, dtype):
+            state[a][name] = kept("%s%d" % (name, a), shape, dtype, TAKES.get("%s%d" % (name, a)))
             return state[a][name]
 
-        def block(b):
-            return slice(b * P, (b + 1) * P)
-
         def round_h(a):
-            h_bf = staged(a, "h_bf", [P, P, PACK], BF16)
-            nc.scalar.copy(h_bf[:], h_banks[a][:].rearrange("p t n -> p n t"))
+            source = h_banks[a][:].rearrange("p t n -> p n t")
+            if a == ROUND_H_ON_VECTOR:
+                state[a]["h_bf"] = placed("h_bf", [P, P, PACK], BF16, LATE + PACK * S)
+                nc.vector.tensor_copy(state[a]["h_bf"][:], source)
+            else:
+                nc.scalar.copy(staged(a, "h_bf", [P, P, PACK], BF16)[:], source)
 
         def inner(a):
-            codes = h_codes[:, block(a)].bitcast(FP8X4)
-            scales = h_scales[:, block(a)]
+            codes = h_codes[:, a * P : (a + 1) * P].bitcast(FP8X4)
+            scales = h_scales[:, a * P : (a + 1) * P]
             nc.vector.quantize_mx(out=codes, scales=scales, in_=state[a]["h_bf"][:].rearrange("p n t -> p (n t)"))
-            state[a]["y"] = []
-            for b in range(V_BLOCKS):
-                y = bank("y", [P, P], Y_BANKS[V_BLOCKS * a + b])
-                state[a]["y"].append(y)
-                nc.tensor.matmul_mx(
-                    out=y[:],
-                    lhsT=codes,
-                    lhsT_scale=scales,
-                    rhs=e_pick[:, block(b)].bitcast(FP8X4),
-                    rhs_scale=es_plane[:, block(b)],
-                    start=True,
-                    stop=True,
-                )
+            state[a]["y"] = bank("y", [P, V], Y_BANKS[a])
+            nc.tensor.matmul_mx(
+                out=state[a]["y"][:],
+                lhsT=codes,
+                lhsT_scale=scales,
+                rhs=e_pick[:].bitcast(FP8X4),
+                rhs_scale=es_plane[:],
+                start=True,
+                stop=True,
+            )
 
         def distance(a):
             part = staged(a, "part", [P, V], F32)
-            for b in range(V_BLOCKS):
-                nc.vector.scalar_tensor_tensor(
-                    part[:, block(b)], state[a]["y"][b][:], -0.2, qn_wide[:, block(b)], ALU.mult, ALU.add
-                )
+            nc.vector.scalar_tensor_tensor(part[:], state[a]["y"][:], -0.2, qn_wide[:], ALU.mult, ALU.add)
 
         def inverse_root(a):
             root = staged(a, "root", [P, V], F32)
-            for b in range(V_BLOCKS):
-                nc.scalar.activation(
-                    root[:, block(b)],
-                    state[a]["part"][:, block(b)],
-                    ACT.Abs_reciprocal_sqrt,
-                    bias=beta[:, a : a + 1],
-                    scale=alpha[:],
-                )
+            nc.scalar.activation(
+                root[:], state[a]["part"][:], ACT.Abs_reciprocal_sqrt, bias=beta[:, a : a + 1], scale=alpha[:]
+            )
+
+        def square(engine, target, source):
+            if engine == "S":
+                nc.scalar.activation(target, source, ACT.Square)
+            elif engine == "V":
+                nc.vector.tensor_tensor(target, source, source, ALU.mult)
+            else:
+                nc.gpsimd.tensor_tensor(target, source, source, ALU.mult)
 
         def kernel_value(a):
             kern = staged(a, "kern", [P, V], F32)
-            for b in range(V_BLOCKS):
-                root = state[a]["root"][:, block(b)]
-                if a in SQUARE_ON_VECTOR:
-                    nc.vector.tensor_tensor(kern[:, block(b)], root, root, ALU.mult)
-                else:
-                    nc.scalar.activation(kern[:, block(b)], root, ACT.Square)
+            square(FIRST[a], kern[:], state[a]["root"][:])
 
         def first_factor(a):
+            kern = state[a]["kern"]
             left = staged(a, "left", [P, V], F32)
-            for b in range(V_BLOCKS):
-                nc.scalar.activation(left[:, block(b)], state[a]["kern"][:, block(b)], ACT.Square)
+            if SECOND[a] == "C":
+                nc.vector.tensor_tensor(left[:], kern[:], c_wide[:], ALU.mult)
+                state[a]["right"] = kern
+            else:
+                square(SECOND[a], left[:], kern[:])
+                state[a]["right"] = c_wide
 
         def weigh(a):
             rr = staged(a, "rr", [P, V], F32)
             rr_sum = staged(a, "rr_sum", [P, 1], F32)
             nc.vector.scalar_tensor_tensor(
-                rr[:], state[a]["left"][:], 1.0, c_wide[:], ALU.mult, ALU.mult, accum_out=rr_sum[:]
+                rr[:], state[a]["left"][:], 1.0, state[a]["right"][:], ALU.mult, ALU.mult, accum_out=rr_sum[:]
             )
 
         def invert(a):
@@ -311,19 +313,20 @@ def tile_picked_ydec_tgt_p_kernel(
 
         def finish(a):
             res = staged(a, "res", [P, V], F32)
-            if a in SCALE_ON_SCALAR:
-                nc.scalar.activation(res[:], state[a]["rr"][:], ACT.Copy, scale=state[a]["norm"][:])
-            else:
-                nc.vector.tensor_scalar_mul(res[:], state[a]["rr"][:], state[a]["norm"][:])
-            nc.sync.dma_start(out[a * P : (a + 1) * P, :], res[:])
+            for cols in ([slice(0, P), slice(P, V)] if a == TILES - 1 else [slice(0, V)]):
+                if SCALE[a] == "S":
+                    nc.scalar.activation(res[:, cols], state[a]["rr"][:, cols], ACT.Copy, scale=state[a]["norm"][:])
+                elif SCALE[a] == "V":
+                    nc.vector.tensor_scalar_mul(res[:, cols], state[a]["rr"][:, cols], state[a]["norm"][:])
+                else:
+                    nc.gpsimd.tensor_scalar(
+                        res[:, cols], state[a]["rr"][:, cols], state[a]["norm"][:], 1.0, ALU.mult, ALU.mult
+                    )
+                nc.sync.dma_start(out[a * P : (a + 1) * P, cols], res[:, cols])
 
-        for stage in (round_h, inner, distance, inverse_root, kernel_value, first_factor):
-            for a in range(TILES):
-                stage(a)
-        for step in range(TILES + 1):
-            if step < TILES:
-                weigh(step)
-            if step > 0:
-                invert(step - 1)
-        for a in range(TILES):
-            finish(a)
+        steps = {"c": round_h, "q": inner, "A": distance, "B": inverse_root, "C": kernel_value, "D": first_factor}
+        steps["E"] = weigh
+        steps["r"] = invert
+        steps["F"] = finish
+        for step in "c0 c1 q0 c2 c3 q1 q2 q3 A0 A1 A2 A3 B0 B1 B2 B3 C0 C1 C2 C3 D0 D1 D2 D3 E0 E1 r0 E2 r1 E3 r2 r3 F0 F1 F2 F3".split():
+            steps[step[0]](int(step[1]))

@@ -39,7 +39,8 @@ SCALE = "SSVV"
 Y_BANKS = (4, 5, 6, 0)
 C_BANK = 7
 LATE = 2 * PACK * T
-ROUND_H_ON_VECTOR = 2
+ROWS_AT = LATE + PACK * W
+ROUND_H_ON_VECTOR = 3
 TAKES = {"norm0":"kern1","norm1":"kern2","norm2":"kern3"}
 
 
@@ -66,13 +67,12 @@ def tile_picked_ydec_tgt_p_kernel(
 
         offs_sb = kept("offs_sb", [P, S // GROUP], U16)
         cen_sb = kept("cen_sb", [P, V // GROUP], U16)
-        rows = kept("rows", [P, V], F32)
-        own_rows = kept("own_rows", [P, P], F32)
+        mass_row = kept("mass_row", [P, V], F32)
         qn_table = placed("qn_table", [P, W], F32, LATE)
         ident = kept("ident", [P, P], F32)
         border = PACK * T
         xs_table = placed("xs_table", [P, T], U8, border - T // 2)
-        es_table = kept("es_table", [P, W], U8)
+        es_table = placed("es_table", [P, W], U8, ROWS_AT + W // 4)
         xs_plane = [kept("xs_plane%d" % g, [P, S], U8) for g in range(PASSES)]
         es_plane = kept("es_plane", [P, V], U8)
         w_raw = [kept("w_raw0", [P, PACK, H], F32)]
@@ -82,8 +82,7 @@ def tile_picked_ydec_tgt_p_kernel(
         nc.vector.memset(as_words(es_table[:]), 0)
         nc.vector.memset(as_words(es_plane[:]), 0)
         nc.vector.memset(as_words(xs_plane[1][:]), 0)
-        nc.vector.memset(own_rows[0 : P - TILES, :], 0.0)
-        nc.vector.memset(rows[0 : P - 2, :], 0.0)
+        nc.vector.memset(mass_row[0:LAST, :], 0.0)
         nc.vector.memset(qn_table[0:LAST, :], 0.0)
         make_identity(nc, ident[:])
 
@@ -101,9 +100,7 @@ def tile_picked_ydec_tgt_p_kernel(
         nc.sync.dma_start(cen_sb[:], cen)
         nc.scalar.dma_start(qn_table[LAST:P, :], qn[0:1, :])
         load_w(0)
-        nc.scalar.dma_start(rows[P - 2 : LAST, :], mass[0:1, :])
-        nc.scalar.dma_start(rows[LAST:P, :], inv[0:1, :])
-        nc.scalar.dma_start(own_rows[P - TILES : P, :], own.rearrange("(a m) o -> a (m o)", m=P))
+        nc.scalar.dma_start(mass_row[LAST:P, :], mass[0:1, :])
         nc.sync.dma_start(as_words(es_table[0:P:ES_STEP, :]), as_words(e_scales[0]))
         load_words(x_table[0], x_words[0])
         xs_pick = kept("xs_pick", [P, S], U8)
@@ -152,39 +149,22 @@ def tile_picked_ydec_tgt_p_kernel(
         qn_mean = kept("qn_mean", [P, 1], F32)
         nc.scalar.activation(qn_abs[:], qn_wide[:], ACT.Abs, scale=1.0 / V, accum_out=qn_mean[:])
 
-        rows_turn = bank("rows_turn", [P, V_BLOCKS, P], 6)
-        turn(rows_turn, rows)
-        cols = kept("cols", [P, V_BLOCKS, 2], F32)
-        nc.scalar.copy(cols[:], rows_turn[:, :, P - 2 : P])
-        mass_spread = bank("mass_spread", [P, V], 2)
-        spread(mass_spread, [cols[:, b, 0:1] for b in range(V_BLOCKS)])
+        size = kept("size", [P, 1], F32)
+        nc.scalar.activation(size[:], qn_mean[:], ACT.Identity, bias=one[:])
+
+        mass_turn = bank("mass_turn", [P, V_BLOCKS, P], 6)
+        turn(mass_turn, mass_row)
+        mass_cols = kept("mass_cols", [P, V_BLOCKS], F32)
+        nc.scalar.copy(mass_cols[:], mass_turn[:, :, LAST])
+        mass_spread = bank("mass_spread", [P, V], 7)
+        spread(mass_spread, [mass_cols[:, b : b + 1] for b in range(V_BLOCKS)])
         mass_abs = kept("mass_abs", [P, V], F32)
         mass_sum = kept("mass_sum", [P, 1], F32)
         nc.scalar.activation(mass_abs[:], mass_spread[:], ACT.Abs, accum_out=mass_sum[:])
         mass_root = kept("mass_root", [P, 1], F32)
         nc.scalar.activation(mass_root[:], mass_sum[:], ACT.Abs_reciprocal_sqrt)
-        mass_sq = kept("mass_sq", [P, V_BLOCKS], F32)
-        nc.scalar.activation(mass_sq[:], cols[:, :, 0], ACT.Square, scale=mass_root[:])
-        c_cols = kept("c_cols", [P, V_BLOCKS], F32)
-        for b in range(V_BLOCKS):
-            nc.scalar.activation(c_cols[:, b : b + 1], mass_sq[:, b : b + 1], ACT.Copy, scale=cols[:, b, 1:2])
-        c_wide = bank("c_wide", [P, V], C_BANK)
-        spread(c_wide, [c_cols[:, b : b + 1] for b in range(V_BLOCKS)])
-
-        own_turn = bank("own_turn", [P, P], 6)
-        nc.tensor.transpose(own_turn[:], own_rows[:], ident[:])
-        own_cols = own_turn[:, P - TILES : P]
-        own_work = kept("own_work", [P, 2, TILES], F32)
-        own1 = own_work[:, 0, :]
-        nc.scalar.activation(own1, own_cols, ACT.Identity, bias=one[:])
-        own_sum = kept("own_sum", [P, 1], F32)
-        nc.scalar.activation(own_work[:, 1, :], own_cols, ACT.Abs, accum_out=own_sum[:])
-        size = kept("size", [P, 1], F32)
-        nc.scalar.activation(size[:], own_sum[:], ACT.Identity, bias=qn_mean[:])
-        alpha = kept("alpha", [P, 1], F32)
-        nc.scalar.activation(alpha[:], size[:], ACT.Abs_reciprocal_sqrt, bias=1.0)
-        beta = kept("beta", [P, TILES], F32)
-        nc.scalar.activation(beta[:], own1, ACT.Copy, scale=alpha[:])
+        mass_sq = kept("mass_sq", [P, V], F32)
+        nc.scalar.activation(mass_sq[:], mass_spread[:], ACT.Square, scale=mass_root[:])
 
         w_codes = []
         w_scales = []
@@ -223,14 +203,19 @@ def tile_picked_ydec_tgt_p_kernel(
                     stop=(g == PASSES - 1 and t == PACK - 1),
                 )
 
-        gather_x(0, 0, S)
         es_pick = kept("es_pick", [P, V], U8, tag="w_bf0")
         nc.vector.tensor_copy(es_pick[:], es_table[:].indirect(cen_sb[:]))
+        gather_x(0, 0, S)
         for j in range(ROWS):
             move_rows(es_plane[j:P:QUAD, :], es_pick[ES_STEP * j : P : QUAD, :])
+        own_sb = placed("own_sb", [P, TILES], F32, ROWS_AT + W // 4)
+        with nc.allow_non_contiguous_dma(reason="one value of own a partition and tile"):
+            nc.sync.dma_start(own_sb[:], own.rearrange("(a p) o -> p (a o)", p=P))
+        inv_sb = placed("inv_sb", [P, V], F32, ROWS_AT + W)
+        nc.sync.dma_start(inv_sb[:], inv)
         for a in range(TILES):
             project(a, 0)
-        quantize_w(1, "mass_sq")
+        quantize_w(1, None)
         for tiles in [[0],[1],[2,3]]:
             gather_x(1, tiles[0] * P, len(tiles) * P)
             for a in tiles:
@@ -294,11 +279,11 @@ def tile_picked_ydec_tgt_p_kernel(
             kern = state[a]["kern"]
             left = staged(a, "left", [P, V], F32)
             if SECOND[a] == "C":
-                nc.vector.tensor_tensor(left[:], kern[:], c_wide[:], ALU.mult)
+                nc.vector.tensor_tensor(left[:], kern[:], state[0]["c"][:], ALU.mult)
                 state[a]["right"] = kern
             else:
                 square(SECOND[a], left[:], kern[:])
-                state[a]["right"] = c_wide
+                state[a]["right"] = state[0]["c"]
 
         def weigh(a):
             rr = staged(a, "rr", [P, V], F32)
@@ -324,9 +309,23 @@ def tile_picked_ydec_tgt_p_kernel(
                     )
                 nc.sync.dma_start(out[a * P : (a + 1) * P, cols], res[:, cols])
 
-        steps = {"c": round_h, "q": inner, "A": distance, "B": inverse_root, "C": kernel_value, "D": first_factor}
+        def late_rows(step):
+            if step == 0:
+                own_cols = own_sb[:]
+                own_abs = kept("own_abs", [P, TILES], F32)
+                own_sum = kept("own_sum", [P, 1], F32)
+                nc.scalar.activation(own_abs[:], own_cols, ACT.Abs, accum_out=own_sum[:])
+                nc.scalar.activation(alpha[:], own_sum[:], ACT.Abs_reciprocal_sqrt, bias=size[:])
+                nc.scalar.activation(beta[:], own_cols, ACT.Identity, scale=alpha[:], bias=alpha[:])
+            else:
+                state[0]["c"] = placed("c_wide", [P, V], F32, LATE + PACK * S)
+                nc.gpsimd.tensor_tensor(state[0]["c"][:], mass_sq[:], inv_sb[:], ALU.mult)
+
+        alpha = kept("alpha", [P, 1], F32)
+        beta = kept("beta", [P, TILES], F32)
+        steps = {"p": late_rows, "c": round_h, "q": inner, "A": distance, "B": inverse_root, "C": kernel_value, "D": first_factor}
         steps["E"] = weigh
         steps["r"] = invert
         steps["F"] = finish
-        for step in "c0 c1 q0 c2 c3 q1 q2 q3 A0 A1 A2 A3 B0 B1 B2 B3 C0 C1 C2 C3 D0 D1 D2 D3 E0 E1 r0 E2 r1 E3 r2 r3 F0 F1 F2 F3".split():
+        for step in "c0 c1 q0 c3 c2 p0 q1 A0 q2 q3 p1 B0 C0 A1 A2 A3 B1 B2 B3 D0 C1 C2 C3 D1 D2 D3 E0 E1 r0 E2 r1 E3 r2 r3 F0 F1 F2 F3".split():
             steps[step[0]](int(step[1]))

from contextlib import ExitStack

import concourse.mybir as mybir
from concourse.masks import make_identity

K, T, S, H, V, W = 1024, 2048, 512, 512, 256, 1024
FLOPS = 2 * K * H * S + 2 * H * S * V

F32 = mybir.dt.float32
BF16 = mybir.dt.bfloat16
I32 = mybir.dt.int32
U32 = mybir.dt.uint32
U16 = mybir.dt.uint16
U8 = mybir.dt.uint8
FP8X4 = mybir.dt.float8_e4m3fn_x4
ALU = mybir.AluOpType
ACT = mybir.ActivationFunctionType

P = 128
PACK = 4
K_PASS = P * PACK
PASSES = K // K_PASS
TILES = S // P
HALF = S // 2
GROUP = 16
QUAD = 32
QUADS = P // QUAD
ROWS = 4
PASS_ROWS = QUADS * ROWS
V_BLOCKS = V // P
LAST = P - 1
XS_ROW = P - QUAD
XS_FIRST = (12, 4)
ES_STEP = P // PASS_ROWS
ROUND_ON_SCALAR = 44
FIRST = "VVVV"
SECOND = "SSSS"
SCALE = "SSVV"
Y_BANKS = (4, 5, 6, 0)
C_BANK = 7
LATE = 2 * PACK * T
ROWS_AT = LATE + PACK * W
ROUND_H_ON_VECTOR = 3
TAKES = {"norm0":"kern1","norm1":"kern2","norm2":"kern3"}


def tile_picked_ydec_tgt_p_kernel(
    tc, x_words, x_scales, w1, e_words, e_scales, qn, own, mass, inv, offs, cen, out
):
    nc = tc.nc
    with ExitStack() as ctx:
        keep = ctx.enter_context(tc.tile_pool(name="keep", bufs=1))
        laid = ctx.enter_context(tc.tile_pool(name="laid", bufs=1))
        psum = ctx.enter_context(tc.psum_pool(name="psum", bufs=1))

        def kept(name, shape, dtype, tag=None):
            return keep.tile(shape, dtype, name=name, tag=tag or name, align_bytes=64)

        def placed(name, shape, dtype, offset):
            return laid.tile(shape, dtype, name=name, align_bytes=64, offset=offset)

        def bank(name, shape, number):
            return psum.tile(shape, F32, name=name, tag="bank%d" % number)

        def as_words(access):
            return access.bitcast(I32)

        offs_sb = kept("offs_sb", [P, S // GROUP], U16)
        cen_sb = kept("cen_sb", [P, V // GROUP], U16)
        mass_row = kept("mass_row", [P, V], F32)
        qn_table = placed("qn_table", [P, W], F32, LATE)
        ident = kept("ident", [P, P], F32)
        border = PACK * T
        xs_table = placed("xs_table", [P, T], U8, border - T // 2)
        es_table = placed("es_table", [P, W], U8, ROWS_AT + W // 4)
        xs_plane = [kept("xs_plane%d" % g, [P, S], U8) for g in range(PASSES)]
        es_plane = kept("es_plane", [P, V], U8)
        w_raw = [kept("w_raw0", [P, PACK, H], F32)]
        x_table = [kept("x_table0", [P, T], U32)]

        nc.gpsimd.memset(as_words(xs_table[0:XS_ROW, :]), 0)
        nc.vector.memset(as_words(es_table[:]), 0)
        nc.vector.memset(as_words(es_plane[:]), 0)
        nc.vector.memset(as_words(xs_plane[1][:]), 0)
        nc.vector.memset(mass_row[0:LAST, :], 0.0)
        nc.vector.memset(qn_table[0:LAST, :], 0.0)
        make_identity(nc, ident[:])

        def load_w(g):
            nc.sync.dma_start(w_raw[g][:], w1[g * K_PASS : (g + 1) * K_PASS, :].rearrange("(p j) c -> p j c", j=PACK))

        def load_words(table, words):
            nc.sync.dma_start(as_words(table[:]), as_words(words.rearrange("p n t -> p (n t)")))

        def move_rows(target, source):
            nc.sync.dma_start(as_words(target), as_words(source))

        nc.sync.dma_start(offs_sb[:], offs)
        nc.scalar.dma_start(as_words(xs_table[XS_ROW:P, :]), as_words(x_scales.rearrange("g r n -> (g r) n")))
        nc.sync.dma_start(cen_sb[:], cen)
        nc.scalar.dma_start(qn_table[LAST:P, :], qn[0:1, :])
        load_w(0)
        nc.scalar.dma_start(mass_row[LAST:P, :], mass[0:1, :])
        nc.sync.dma_start(as_words(es_table[0:P:ES_STEP, :]), as_words(e_scales[0]))
        load_words(x_table[0], x_words[0])
        xs_pick = kept("xs_pick", [P, S], U8)
        nc.vector.tensor_copy(xs_pick[:], xs_table[:].indirect(offs_sb[:]))

        nc.vector.tensor_copy(as_words(xs_plane[0][:]), as_words(xs_pick[:]))

        def move_quadrant(q):
            row = QUAD * q + XS_FIRST[0]
            move_rows(xs_plane[0][row : row + ROWS, :], xs_pick[XS_ROW + ROWS * q : XS_ROW + ROWS * (q + 1), :])

        for q in range(QUADS - 1):
            move_quadrant(q)
        w_raw.append(placed("w_raw1", [P, PACK, H], F32, 0))
        load_w(1)
        x_table.append(placed("x_table1", [P, T], U32, border))
        load_words(x_table[1], x_words[1])
        for j in range(ROWS):
            move_rows(xs_plane[1][XS_FIRST[1] + j : P : QUAD, :], xs_pick[XS_ROW + PASS_ROWS + j : P : ROWS, :])

        qn_pick = kept("qn_pick", [P, V], F32)
        nc.vector.tensor_copy(qn_pick[:], qn_table[:].indirect(cen_sb[:]))

        def turn(target, source):
            for b in range(V_BLOCKS):
                nc.tensor.transpose(target[:, b, :], source[:, b * P : (b + 1) * P], ident[:])

        def spread(target, columns):
            for b in range(V_BLOCKS):
                nc.tensor.transpose(target[:, b * P : (b + 1) * P], columns[b].to_broadcast([P, P]), ident[:])

        ones = kept("ones", [P, 1], F32)
        nc.vector.memset(ones[:], 1.0)
        one = kept("one", [P, 1], F32)
        nc.scalar.activation(one[:], ones[:], ACT.Abs_reciprocal_sqrt)

        qn_turn = bank("qn_turn", [P, V_BLOCKS, P], 4)
        turn(qn_turn, qn_pick)
        qn_cols = kept("qn_cols", [P, V_BLOCKS], F32)
        nc.scalar.copy(qn_cols[:], qn_turn[:, :, LAST])
        qn_spread = bank("qn_spread", [P, V], 5)
        spread(qn_spread, [qn_cols[:, b : b + 1] for b in range(V_BLOCKS)])
        qn_wide = kept("qn_wide", [P, V], F32)
        nc.scalar.copy(qn_wide[:], qn_spread[:])
        qn_abs = kept("qn_abs", [P, V], F32)
        qn_mean = kept("qn_mean", [P, 1], F32)
        nc.scalar.activation(qn_abs[:], qn_wide[:], ACT.Abs, scale=1.0 / V, accum_out=qn_mean[:])

        size = kept("size", [P, 1], F32)
        nc.scalar.activation(size[:], qn_mean[:], ACT.Identity, bias=one[:])

        mass_turn = bank("mass_turn", [P, V_BLOCKS, P], 6)
        turn(mass_turn, mass_row)
        mass_cols = kept("mass_cols", [P, V_BLOCKS], F32)
        nc.scalar.copy(mass_cols[:], mass_turn[:, :, LAST])
        mass_spread = bank("mass_spread", [P, V], 7)
        spread(mass_spread, [mass_cols[:, b : b + 1] for b in range(V_BLOCKS)])
        mass_abs = kept("mass_abs", [P, V], F32)
        mass_sum = kept("mass_sum", [P, 1], F32)
        nc.scalar.activation(mass_abs[:], mass_spread[:], ACT.Abs, accum_out=mass_sum[:])
        mass_root = kept("mass_root", [P, 1], F32)
        nc.scalar.activation(mass_root[:], mass_sum[:], ACT.Abs_reciprocal_sqrt)
        mass_sq = kept("mass_sq", [P, V], F32)
        nc.scalar.activation(mass_sq[:], mass_spread[:], ACT.Square, scale=mass_root[:])

        w_codes = []
        w_scales = []

        def quantize_w(g, tag):
            w_bf = kept("w_bf%d" % g, [P, PACK * H], BF16, tag=tag)
            dst = w_bf[:].rearrange("p (t m j) -> p m j t", t=PACK, j=PACK)
            src = w_raw[g][:].rearrange("p j (m t) -> p m j t", t=PACK)
            nc.scalar.copy(dst[:, 0:ROUND_ON_SCALAR], src[:, 0:ROUND_ON_SCALAR])
            nc.vector.tensor_copy(dst[:, ROUND_ON_SCALAR:P], src[:, ROUND_ON_SCALAR:P])
            w_codes.append(kept("w_codes%d" % g, [P, H], U32))
            w_scales.append(kept("w_scales%d" % g, [P, H], U8))
            nc.vector.quantize_mx(out=w_codes[g][:].bitcast(FP8X4), scales=w_scales[g][:], in_=w_bf[:])

        quantize_w(0, None)
        e_table = placed("e_table", [P, W], U32, LATE)
        load_words(e_table, e_words[0])

        h_banks = [bank("h", [P, PACK, P], a) for a in range(TILES)]
        x_pick = [kept("x_pick%d" % g, [P, S], U32) for g in range(PASSES)]

        def gather_x(g, n, count=HALF):
            nc.vector.tensor_copy(
                x_pick[g][:, n : n + count], x_table[g][:].indirect(offs_sb[:, n // GROUP : (n + count) // GROUP])
            )

        def project(a, g):
            for t in range(PACK):
                nc.tensor.matmul_mx(
                    out=h_banks[a][:, t, :],
                    lhsT=w_codes[g][:, t * P : (t + 1) * P].bitcast(FP8X4),
                    lhsT_scale=w_scales[g][:, t * P : (t + 1) * P],
                    rhs=x_pick[g][:, a * P : (a + 1) * P].bitcast(FP8X4),
                    rhs_scale=xs_plane[g][XS_FIRST[g] : P, a * P : (a + 1) * P],
                    start=(g == 0 and t == 0),
                    stop=(g == PASSES - 1 and t == PACK - 1),
                )

        es_pick = kept("es_pick", [P, V], U8, tag="w_bf0")
        nc.vector.tensor_copy(es_pick[:], es_table[:].indirect(cen_sb[:]))
        gather_x(0, 0, S)
        for j in range(ROWS):
            move_rows(es_plane[j:P:QUAD, :], es_pick[ES_STEP * j : P : QUAD, :])
        own_sb = placed("own_sb", [P, TILES], F32, ROWS_AT + W // 4)
        with nc.allow_non_contiguous_dma(reason="one value of own a partition and tile"):
            nc.sync.dma_start(own_sb[:], own.rearrange("(a p) o -> p (a o)", p=P))
        inv_sb = placed("inv_sb", [P, V], F32, ROWS_AT + W)
        nc.sync.dma_start(inv_sb[:], inv)
        for a in range(TILES):
            project(a, 0)
        quantize_w(1, None)
        for tiles in [[0],[1],[2,3]]:
            gather_x(1, tiles[0] * P, len(tiles) * P)
            for a in tiles:
                project(a, 1)
        e_pick = kept("e_pick", [P, V], U32)
        nc.vector.tensor_copy(e_pick[:], e_table[:].indirect(cen_sb[:]))
        h_codes = placed("h_codes", [P, S], U32, LATE)
        h_scales = kept("h_scales", [P, S], U8)
        state = [dict() for a in range(TILES)]

        def staged(a, name, shape, dtype):
            state[a][name] = kept("%s%d" % (name, a), shape, dtype, TAKES.get("%s%d" % (name, a)))
            return state[a][name]

        def round_h(a):
            source = h_banks[a][:].rearrange("p t n -> p n t")
            if a == ROUND_H_ON_VECTOR:
                state[a]["h_bf"] = placed("h_bf", [P, P, PACK], BF16, LATE + PACK * S)
                nc.vector.tensor_copy(state[a]["h_bf"][:], source)
            else:
                nc.scalar.copy(staged(a, "h_bf", [P, P, PACK], BF16)[:], source)

        def inner(a):
            codes = h_codes[:, a * P : (a + 1) * P].bitcast(FP8X4)
            scales = h_scales[:, a * P : (a + 1) * P]
            nc.vector.quantize_mx(out=codes, scales=scales, in_=state[a]["h_bf"][:].rearrange("p n t -> p (n t)"))
            state[a]["y"] = bank("y", [P, V], Y_BANKS[a])
            nc.tensor.matmul_mx(
                out=state[a]["y"][:],
                lhsT=codes,
                lhsT_scale=scales,
                rhs=e_pick[:].bitcast(FP8X4),
                rhs_scale=es_plane[:],
                start=True,
                stop=True,
            )

        def distance(a):
            part = staged(a, "part", [P, V], F32)
            nc.vector.scalar_tensor_tensor(part[:], state[a]["y"][:], -0.2, qn_wide[:], ALU.mult, ALU.add)

        def inverse_root(a):
            root = staged(a, "root", [P, V], F32)
            nc.scalar.activation(
                root[:], state[a]["part"][:], ACT.Abs_reciprocal_sqrt, bias=beta[:, a : a + 1], scale=alpha[:]
            )

        def square(engine, target, source):
            if engine == "S":
                nc.scalar.activation(target, source, ACT.Square)
            elif engine == "V":
                nc.vector.tensor_tensor(target, source, source, ALU.mult)
            else:
                nc.gpsimd.tensor_tensor(target, source, source, ALU.mult)

        def kernel_value(a):
            kern = staged(a, "kern", [P, V], F32)
            square(FIRST[a], kern[:], state[a]["root"][:])

        def first_factor(a):
            kern = state[a]["kern"]
            left = staged(a, "left", [P, V], F32)
            if SECOND[a] == "C":
                nc.vector.tensor_tensor(left[:], kern[:], state[0]["c"][:], ALU.mult)
                state[a]["right"] = kern
            else:
                square(SECOND[a], left[:], kern[:])
                state[a]["right"] = state[0]["c"]

        def weigh(a):
            rr = staged(a, "rr", [P, V], F32)
            rr_sum = staged(a, "rr_sum", [P, 1], F32)
            nc.vector.scalar_tensor_tensor(
                rr[:], state[a]["left"][:], 1.0, state[a]["right"][:], ALU.mult, ALU.mult, accum_out=rr_sum[:]
            )

        def invert(a):
            norm = staged(a, "norm", [P, 1], F32)
            nc.vector.reciprocal(norm[:], state[a]["rr_sum"][:])

        def finish(a):
            res = staged(a, "res", [P, V], F32)
            for cols in ([slice(0, P), slice(P, V)] if a == TILES - 1 else [slice(0, V)]):
                if SCALE[a] == "S":
                    nc.scalar.activation(res[:, cols], state[a]["rr"][:, cols], ACT.Copy, scale=state[a]["norm"][:])
                elif SCALE[a] == "V":
                    nc.vector.tensor_scalar_mul(res[:, cols], state[a]["rr"][:, cols], state[a]["norm"][:])
                else:
                    nc.gpsimd.tensor_scalar(
                        res[:, cols], state[a]["rr"][:, cols], state[a]["norm"][:], 1.0, ALU.mult, ALU.mult
                    )
                nc.sync.dma_start(out[a * P : (a + 1) * P, cols], res[:, cols])

        def late_rows(step):
            if step == 0:
                own_cols = own_sb[:]
                own_abs = kept("own_abs", [P, TILES], F32)
                own_sum = kept("own_sum", [P, 1], F32)
                nc.scalar.activation(own_abs[:], own_cols, ACT.Abs, accum_out=own_sum[:])
                nc.scalar.activation(alpha[:], own_sum[:], ACT.Abs_reciprocal_sqrt, bias=size[:])
                nc.scalar.activation(beta[:], own_cols, ACT.Identity, scale=alpha[:], bias=alpha[:])
            else:
                state[0]["c"] = placed("c_wide", [P, V], F32, LATE + PACK * S)
                nc.gpsimd.tensor_tensor(state[0]["c"][:], mass_sq[:], inv_sb[:], ALU.mult)

        alpha = kept("alpha", [P, 1], F32)
        beta = kept("beta", [P, TILES], F32)
        steps = {"p": late_rows, "c": round_h, "q": inner, "A": distance, "B": inverse_root, "C": kernel_value, "D": first_factor}
        steps["E"] = weigh
        steps["r"] = invert
        steps["F"] = finish
        for step in "c0 c1 q0 c3 c2 p0 q1 A0 q2 q3 p1 B0 C0 A1 A2 A3 B1 B2 B3 D0 C1 C2 C3 D1 D2 D3 E0 E1 r0 E2 r1 E3 r2 r3 F0 F1 F2 F3".split():
            steps[step[0]](int(step[1]))
